import numpy as np, ml_dtypes
CORES = [242,247,114,119]
N = 4
BF = ml_dtypes.bfloat16
V, S, P, SH, RO = 1024, 10, 8, 4, 3
M, K1, K2, K3, K4, K5 = 4096, 1597, 613, 911, 1223, 74
def pack(s, li):
    return {"x": np.ascontiguousarray(s.reshape(N, 128, V)).astype(np.float32).astype(BF), "liar": np.ascontiguousarray(li).astype(np.int32)}
def states(rng):
    mid = rng.integers(30, 226, (N, 8, 16, 1)); wid = rng.integers(15, 90, (N, 8, 1, 1))
    return np.clip(np.rint(mid + wid * rng.standard_normal((N, 8, 16, V))), 0, 255).astype(np.int64)
def lies(rng, s, li):
    kind = rng.integers(0, 3, (N, 8, 1, V))
    w = np.where(kind == 0, 255 * rng.integers(0, 2, s.shape), np.where(kind == 1, 255 * rng.integers(0, 2, (N, 8, 1, V)), rng.integers(0, 256, s.shape)))
    return np.where(li[:, :, None, :], w, s)
def hit(u):
    return ((u * u >> 7) + u) & (M - 1)
def draws(i, c, t):
    m = np.arange(S, dtype=np.int64)[:, None]
    return hit((i * K1 + c * (K2 + K5 * m) + t * K3 + m * K4) & (M - 1))
def comps(rng, c):
    r = np.clip(np.rint(c[:, None, :] * 0.0625 + 50 * rng.standard_normal((8, 16, M))), 0, 255).astype(np.int64)
    left = c - np.add.reduce(r, axis=1)
    for i in rng.permutation(16):
        a = np.clip(left, -r[:, i], 255 - r[:, i]); r[:, i] += a; left = left - a
    return r
def steered(rng, us, m):
    c = np.full(M, M, np.int64); back = pow(K2 + K5 * m, 1023, M)
    for k in range(12):
        w = us[rng.integers(0, len(us), M)]
        c = np.where(c > 4080, ((w - np.arange(M, dtype=np.int64) * K1 - m * K4) * back) & (M - 1), c)
    return np.minimum(c, 4080)
def placed(u, d):
    c = (((d - K4) >> 1) * pow(K5 >> 1, 1023, 2048)) & 2047
    c = np.concatenate([c, c + 2048]); u = np.concatenate([u, u]); k = c <= 4080; c = c[k]; u = u[k]
    return ((u - c * K2) * pow(K1, 1023, M)) & (M - 1), c
def thrice():
    u = np.arange(M, dtype=np.int64); h = hit(u).astype(np.int16); us, ds = [], []
    for a in range(0, M // 2, 128):
        d = 2 * np.arange(a, a + 128, dtype=np.int64)[:, None] + 1; n = np.zeros((128, M), np.int8)
        for k in range(1, min(S, 8)): n += (h[(u + k * d) & (M - 1)] == h)
        j, i = np.nonzero(n >= 2); us.append(u[i]); ds.append(d[j, 0])
    return np.concatenate(us), np.concatenate(ds)
def twice():
    u = np.arange(M, dtype=np.int64); h = hit(u); n = np.zeros((M, M), np.int8)
    for m in range(S): n[h, ((u - h * K1 - m * K4) * pow(K2 + K5 * m, 1023, M)) & (M - 1)] += 1
    return np.nonzero(n[:, :4081] >= 2)
def some(rng, a):
    e = rng.permutation(len(a[0]))[:48]
    return a[0][e], a[1][e]
def setup_inputs(rng):
    s = states(rng); li = rng.random((N, 8, V)) < rng.choice(np.array([0.03, 0.1, 0.2, 0.35]), (N, 8, 1))
    return pack(lies(rng, s, li), li)
def setup_inputs_alike(rng):
    s = states(rng); li = rng.random((N, 8, V)) < 0.1; o = rng.permutation(8)
    for g in (o[0], o[1]): li[:, g] = False
    s = lies(rng, s, li)
    s[:, o[0]] = rng.integers(0, 256, (16, 1))
    s[:, o[1]] = rng.integers(0, 255, (16, 1)) + rng.integers(0, 2, (N, 16, V))
    s[:, o[2]] = 255 * rng.integers(0, 2, (N, 16, V))
    a = rng.integers(0, 256, (2, 16, 1)); s[:, o[3]] = np.where(rng.random((N, 1, V)) < 0.5, a[0], a[1])
    s[:, o[4]] = np.where(li[:, o[4]][:, None, :], s[:, o[4]], rng.integers(0, 256, (16, 1)))
    return pack(s, li)
def setup_inputs_ends(rng):
    s = states(rng); li = rng.random((N, 8, V)) < 0.1; s = lies(rng, s, li)
    k = rng.integers(0, 8, (N, 8, 1, V)); s = np.where(k == 0, 0, np.where(k == 1, 255, s))
    s[:, ::2, :, 0] = 255; s[:, 1::2, :, 0] = 0; s[:, ::2, :, V - 1] = 0; s[:, 1::2, :, V - 1] = 255
    li[0, :, 0] = True; li[N - 1, :, V - 1] = True; li[0, :, V - 1] = False; li[N - 1, :, 0] = False
    return pack(s, li)
def setup_inputs_liars(rng):
    s = states(rng); li = rng.random((N, 8, V)) < 0.25; o = rng.permutation(8)
    li[:, o[0]] = False; li[:, o[1]] = True
    i = int(rng.integers(0, M)); li[:, o[2]] = True; li[i // V, o[2], i % V] = False
    li[:, o[3]] = False; li[rng.integers(0, N), o[3], rng.integers(0, V)] = True
    li[:, o[4]] = False; li[rng.integers(0, N), o[4]] = True
    li[:, o[5]] = False; li[:, o[5], ::2] = True
    li[:, o[6]] = False; li[:, o[6], V // 4:V // 2] = True
    s = lies(rng, s, li)
    b = rng.integers(0, 256, 16); s[i // V, o[2], :, i % V] = b
    for p in draws(np.array([i]), np.array([int(np.sum(b))]), 0)[:, 0]: s[int(p) // V, o[2], :, int(p) % V] = b
    return pack(s, li)
def setup_inputs_steer(rng):
    o = rng.permutation(8); h = hit(np.arange(M, dtype=np.int64)); q = rng.permutation(N)
    c = rng.integers(0, 4081, (8, M)); li = rng.random((8, M)) < 0.1; li[o[0]] = False
    top = np.flatnonzero(np.bincount(h, minlength=M) >= 4)
    for g, m in ((o[0], 0), (o[1], S - 1), (o[2], int(rng.integers(0, S)))): c[g] = steered(rng, np.flatnonzero(h == rng.choice(top)), m)
    for g, w in ((o[3], q[0]), (o[4], q[1])): c[g] = steered(rng, np.flatnonzero(h // V == w), int(rng.integers(0, S)))
    self2 = twice(); three = placed(*thrice()); close = placed(np.arange(4, dtype=np.int64), np.ones(4, np.int64))
    for j in range(3):
        g = o[5 + j]; li[g] = rng.random(M) < 0.5
        a = [some(rng, close), some(rng, self2), some(rng, three)]
        for i, k in a[1:]:
            p = draws(i, k, 0); c[g, p] = rng.integers(0, 300, p.shape)
        p = draws(a[2][0], a[2][1], 0)[0]; c[g, p] = rng.integers(3600, 4081, p.shape)
        for i, k in a[j + 1:] + a[:j + 1]:
            c[g, i] = k; li[g, i] = False
    s = comps(rng, c)
    return pack(np.ascontiguousarray(s.reshape(8, 16, N, V).transpose(2, 0, 1, 3)), li.reshape(8, N, V).transpose(1, 0, 2))
def setup_inputs_spread(rng):
    s = np.floor(np.exp2(8 * rng.random((N, 8, 1, V))) * rng.random((N, 8, 16, V))).astype(np.int64)
    s = np.clip(np.where(rng.random((N, 8, 1, 1)) < 0.4, 255 - s, s), 0, 255)
    li = rng.random((N, 8, V)) < 0.5 * rng.random((N, 8, 1))
    q = rng.permutation(N); li[q[0]] = False; li[q[1]] = True
    return pack(s, li)
def check_inputs(d):
    bad = []
    v = d["x"].astype(np.float32)
    if not np.all((v >= 0) & (v <= 255) & (v == np.floor(v))): bad.append("range of x")
    if np.min(d["liar"]) < 0 or np.max(d["liar"]) > 1: bad.append("range of liar")
    return bad
def reference(x, liar):
    s = np.ascontiguousarray(x.astype(np.float32).astype(np.int32).reshape(N, 8, 16, V).transpose(1, 2, 0, 3)).reshape(8, 16, M)
    stay = np.ascontiguousarray(liar.transpose(1, 0, 2)).reshape(8, 1, M) == 1
    ids = np.arange(M, dtype=np.int64)
    for t in range(RO):
        c = np.add.reduce(s.astype(np.int64), axis=1)
        tot, hi, lo = 0, 0, 255
        for m in range(S):
            u = (ids * K1 + c * (K2 + K5 * m) + t * K3 + m * K4) & (M - 1)
            peer = ((u * u >> 7) + u) & (M - 1)
            v = np.take_along_axis(s, peer[:, None, :], 2)
            tot = tot + v; hi = np.maximum(hi, v); lo = np.minimum(lo, v)
        s = np.where(stay, s, (tot - hi - lo + P * s) >> SH)
    y = np.ascontiguousarray(s.reshape(8, 16, N, V).transpose(2, 0, 1, 3)).reshape(N, 128, V)
    return {"y": y.astype(np.float32).astype(BF)}

@@ -1,0 +1,337 @@
+from concourse.bass import DstId, RemoteDMATransfer
+from concourse.mybir import AluOpType, ActivationFunctionType
+
+V, S, M, RO = 1024, 10, 4096, 3
+K1, K2, K3, K4, K5 = 1597, 613, 911, 1223, 74
+CHUNKS = [160, 256, 192, 144, 112, 80, 48, 32]
+GROUPS = [[0, 1], [2, 3], [4, 5, 6, 7]]
+LAST_GROUPS = [[0, 1], [2, 3], [4, 5], [6, 7]]
+RELAY = 0
+NMAX = max(CHUNKS)
+MAGIC = 12582912.0
+RESET = 264.5
+COLS = V * S // 16
+ORDER = "ra0 ra1 rb0 rb1 ym0 ym1 sq0 ra2 su0 rb2 sq1 su1 za0 ym2 zb0 za1 zc0 sq2 su2 zb1 za2 zc1 zb2 zc2".split()
+ORDER0 = "ra0 rb0 ym0 ra1 sq0 rb1 su0 ym1 ra2 sq1 rb2 su1 za0 ym2 zb0 za1 zc0 sq2 su2 zb1 za2 zc1 zb2 zc2".split()
+
+SCRATCH = {}
+for _names, _spec in [
+        ("w0 w1 w2", ("sbuf", [128, M], "bfloat16")),
+        ("res lb", ("sbuf", [128, V], "bfloat16")),
+        ("vals", ("sbuf", [128, V * S], "bfloat16")),
+        ("his los", ("sbuf", [128, V * S], "float16")),
+        ("dseg", ("sbuf", [128, NMAX * S + 16], "float16")),
+        ("band", ("sbuf", [128, 8, 40], "float16")),
+        ("wk", ("sbuf", [128, 12, 128], "float16")),
+        ("pi pj", ("sbuf", [128, 4], "int32")),
+        ("pf pc", ("sbuf", [128, 4], "float32")),
+        ("e5 ee a5 b5 bcol lcol", ("sbuf", [128, 8], "float32")),
+        ("n8", ("sbuf", [128, 8], "int32")),
+        ("m16", ("sbuf", [128, 16], "float32")),
+        ("g16 kk bm", ("sbuf", [128, 8, S], "float32")),
+        ("jp i32", ("sbuf", [128, 128], "float32")),
+        ("i16 ih", ("sbuf", [128, 128], "bfloat16")),
+        ("in16", ("sbuf", [128, 128], "float16")),
+        ("li", ("sbuf", [128, V // 16], "int32")),
+        ("lf", ("sbuf", [128, V // 16], "bfloat16")),
+        ("lc lt base0 base1 base2 qq yy", ("sbuf", [128, COLS], "float32")),
+        ("zi zj", ("sbuf", [128, COLS], "int32")),
+        ("off", ("sbuf", [128, COLS], "uint16")),
+        ("f0 f1 f2 f3 x0 x1 x2", ("psum", [128, 512], "float32"))]:
+    for _n in _names.split():
+        SCRATCH[_n] = _spec
+SEMAPHORES = (["u%d" % i for i in range(48)]
+              + ["ga%d" % i for i in range(len(CHUNKS))] + ["sc%d" % i for i in range(len(CHUNKS))]
+              + ["pe%d" % i for i in range(4)] + ["fin%d" % i for i in range(4)]
+              + ["%s%d" % (a, i) for a in ("xm", "ra", "rb", "ym", "sq", "su", "za", "zb", "zc") for i in range(3)]
+              + ["hop%d" % i for i in range(4)] + ["loadx%d" % i for i in range(4)]
+              + ["arr0", "arr1", "arr2", "sent", "loadl", "stored"])
+
+SEGS = [(c5, n8, 15 + 16 * c5 - S * n8) for c5 in range(5) for n8 in range(8) if -15 <= 16 * c5 - S * n8 <= S - 1]
+
+
+def engine_split(src, peers, topo):
+    near = [d for d in peers if d in topo.cores_of(src)]
+    far = [d for d in peers if d not in near]
+    out = {}
+    used = []
+    for i, d in enumerate(far):
+        es = topo.engines(src, d)
+        n = len(es) // len(far)
+        out[d] = es[i * n:(i + 1) * n]
+        used += es
+    for i, d in enumerate(near):
+        es = [e for e in topo.engines(src, d) if e not in used]
+        n = len(es) // len(near)
+        out[d] = es[i * n:(i + 1) * n]
+    return out
+
+
+def rank_program(g, core, T, topo):
+    rank = T.rank_of(core)
+    if rank is None:
+        return
+    A = AluOpType
+    F = ActivationFunctionType
+    ve, ac, pe, sy = g.vector, g.scalar, g.tensor, g.sync
+    queues = {"g": g, "v": ve, "a": ac, "p": pe, "s": sy}
+    count, seen, fresh = {}, {}, [0]
+
+    def done(ins, name=None, n=1):
+        if name is None:
+            name = "u%d" % fresh[0]
+            fresh[0] += 1
+        ins.then_inc(T.sem[name], n)
+        count[name] = count.get(name, 0) + n
+        return (name, count[name])
+
+    def wait(q, *toks):
+        for name, n in toks:
+            if seen.get((q, name), 0) < n:
+                queues[q].wait_ge(T.sem[name], n)
+                seen[(q, name)] = n
+
+    peers = [c for c in T.cores if c != core]
+    split = engine_split(core, peers, topo)
+    landing = sum(len(engine_split(c, [d for d in T.cores if d != c], topo)[core]) for c in peers)
+    own = rank * V
+    wins = [T.w0, T.w1, T.w2]
+    bases = [T.base0, T.base1, T.base2]
+    fb = [T.f0, T.f1, T.f2, T.f3]
+    xb = [T.x0, T.x1, T.x2]
+    starts = [sum(CHUNKS[:i]) for i in range(len(CHUNKS) + 1)]
+    parts = [(starts[gr[0]], starts[gr[-1] + 1]) for gr in GROUPS]
+    part_of = {i: k for k, gr in enumerate(GROUPS) for i in gr}
+
+    def send(ap, plan):
+        trs = []
+        for d, es, sem in plan:
+            rid, pid = topo.addr(d, core)
+            trs.append(RemoteDMATransfer(dst_ids=[DstId(rid=rid, pnc=pid)], dma_engine_mask=sum(1 << e for e in es),
+                                         remote_sem=T.sem[sem], src=ap, dst=ap))
+        g.remote_dma_fused(trs, local_sem=T.sem.sent)
+        count["sent"] = count.get("sent", 0) + sum(len(es) for d, es, sem in plan)
+
+    pieces = max(RELAY, 1)
+    pw = V // pieces
+    t_x = [done(sy.dma_start(T.w0[:, own + j * pw:own + (j + 1) * pw], T.x[:, j * pw:(j + 1) * pw]), "loadx%d" % j, 16)
+           for j in range(pieces)]
+    t_l = done(ac.dma_start(T.li[:], T.liar[:]), "loadl", 16)
+    fl = {"allow_small_or_imprecise_dtypes": True}
+    t_pi = done(g.iota(T.pi[:, 0:1], [[0, 1]], 0, 1))
+    t_e5 = done(g.iota(T.e5[:, 0:5], [[16, 5]], 0, 0, **fl))
+    t_g16 = done(g.iota(T.g16[:], [[16, 8], [0, S]], 0, 0, **fl))
+    t_kk = done(g.iota(T.kk[:], [[0, 8], [K5, S]], K2, 0, **fl))
+    t_jp = done(g.iota(T.jp[:], [[1, 128]], 0, -1, **fl))
+    if RELAY:
+        near = [d for d in peers if d in topo.cores_of(core)][0]
+        twin = [d for d in peers if d != near and topo.die(d) == topo.die(core)][0]
+        two = engine_split(core, [near, twin], topo)
+        first = []
+        for j in range(pieces):
+            wait("g", t_x[j])
+            send(T.w0[:, own + j * pw:own + (j + 1) * pw], [(twin, two[twin], "hop%d" % j), (near, two[near], "arr0")])
+            first.append(("hop%d" % j, len(two[twin])))
+        o2 = T.rank_of(twin) * V
+        on = topo.engines(core, near)
+        for j in range(pieces):
+            wait("g", first[j])
+            send(T.w0[:, o2 + j * pw:o2 + (j + 1) * pw], [(near, on, "arr0")])
+        first.append(("arr0", pieces * (len(two[near]) + len(on))))
+    else:
+        wait("g", t_x[0])
+        send(T.w0[:, own:own + V], [(d, split[d], "arr0") for d in peers])
+        first = [("arr0", landing)]
+
+    t_z0 = done(ve.memset(T.band[:], 0.0))
+    t_d0 = done(ve.memset(T.dseg[:], 0.0))
+    wait("v", t_pi)
+    ta = done(ve.tensor_scalar(T.pj[:, 0:1], T.pi[:, 0:1], 15, None, A.bitwise_and), "u47")
+    ta = done(ve.tensor_scalar(T.pj[:, 1:2], T.pi[:, 0:1], 112, None, A.bitwise_and), "u47")
+    step = (8 * K1) % M
+    c0 = (K1 * own) % M - 2047.5
+    tb = done(ve.tensor_scalar(T.pc[:, 0:1], T.pi[:, 0:1], step / M, c0 / M, A.mult, A.add), "u46")
+    tb = done(ve.tensor_scalar(T.pc[:, 1:2], T.pi[:, 0:1], 1024.0, float(2 ** 25 + 128 * own), A.mult, A.add), "u46")
+    wait("v", ta)
+    t_pf = done(ve.tensor_copy(T.pf[:, 0:2], T.pj[:, 0:2]))
+    wait("v", t_pf, t_e5)
+    t_ee = done(ve.tensor_scalar(T.ee[:, 0:5], T.e5[:, 0:5], T.pf[:, 0:1], None, A.add))
+    wait("v", t_g16)
+    t_bm = done(ve.tensor_scalar(T.bm[:], T.g16[:], T.pf[:, 1:2], 1.0 / M, A.is_equal, A.mult))
+    wait("v", t_ee, tb)
+    t_n8 = done(ve.tensor_scalar(T.n8[:, 0:5], T.ee[:, 0:5], -4.5, 0.1, A.add, A.mult))
+    t_a5 = done(ve.tensor_scalar(T.a5[:, 0:5], T.ee[:, 0:5], K4 / M, T.pc[:, 0:1], A.mult, A.add))
+    wait("v", t_bm, t_kk, t_z0)
+    t_band = done(ve.tensor_tensor(T.band[:, :, 15:15 + S], T.bm[:], T.kk[:], A.mult))
+    wait("v", t_n8)
+    t_b5 = done(ve.tensor_scalar(T.b5[:, 0:5], T.n8[:, 0:5], (K1 - S * K4) / M, None, A.mult))
+    t_lcol = done(ve.tensor_scalar(T.lcol[:, 0:5], T.n8[:, 0:5], 128.0, T.pc[:, 1:2], A.mult, A.add))
+    wait("v", t_jp)
+    t_m16 = done(ve.tensor_scalar(T.m16[:], T.jp[:, 0:16], T.pf[:, 1:2], 0.0, A.add, A.is_equal))
+    wait("v", t_a5, t_b5)
+    t_bcol = done(ve.tensor_tensor(T.bcol[:, 0:5], T.a5[:, 0:5], T.b5[:, 0:5], A.add))
+    t_i32 = done(ve.tensor_scalar(T.i32[:], T.jp[:], 0.0, None, A.is_equal))
+    wait("v", t_band)
+    for s, (c5, n8, o) in enumerate(SEGS):
+        t_wk = done(ve.tensor_copy(T.wk[:, s, :], T.band[:, :, o:o + 16]), "u45")
+    wait("v", t_l, t_m16)
+    t_lf = done(ve.tensor_scalar(T.lf[:], T.li[:], float(2 ** 30), None, A.mult))
+    wait("v", t_lcol)
+    for c5 in range(5):
+        t_lc = done(ve.tensor_scalar(T.lc[:, c5::5], T.jp[:], 1024.0, T.lcol[:, c5:c5 + 1], A.mult, A.add), "u43")
+    wait("v", t_lf)
+    for a in range(8, 16):
+        t_lb2 = done(ve.tensor_scalar(T.lb[:, 64 * a:64 * a + 64], T.lf[:], T.m16[:, a:a + 1], None, A.mult), "u37")
+
+    wait("a", t_bcol, t_jp)
+    for c5 in range(5):
+        t_base0 = done(ac.activation(T.base0[:, c5::5], T.jp[:], F.Identity, bias=T.bcol[:, c5:c5 + 1], scale=step / M), "u44")
+    wait("a", t_lf, t_m16)
+    for a in range(8):
+        t_lb = done(ac.activation(T.lb[:, 64 * a:64 * a + 64], T.lf[:], F.Identity, scale=T.m16[:, a:a + 1]), "u38")
+    t_base = [t_base0, None, None]
+
+    def base_mm(t, k):
+        n0, n1 = parts[k]
+        c, w = 5 * n0 // 8, 5 * (n1 - n0) // 8
+        wait("p", t_base[t], t_i32)
+        pe.matmul(xb[k][:, 0:w], T.i32[:], bases[t][:, c:c + w], True, False)
+
+    def x_mm(t, k, *toks):
+        n0, n1 = parts[k]
+        w = 5 * (n1 - n0) // 8
+        wait("p", t_wk, *toks)
+        for s, (c5, n8, o) in enumerate(SEGS):
+            ins = pe.matmul(xb[k][:, c5:w:5], T.wk[:, s, :], wins[t][:, own + n0 + n8:own + n1:8],
+                            False, s == len(SEGS) - 1)
+        return done(ins, "xm%d" % k)
+
+    def peers_from(t_xm, order, before_za):
+        tk = {}
+        extra = None
+        for name in order:
+            s, k = name[:2], int(name[2])
+            c, w = 5 * parts[k][0] // 8, 5 * (parts[k][1] - parts[k][0]) // 8
+            px = xb[k][:, 0:w]
+            if s == "ra":
+                wait("a", t_xm[k])
+                ins = ac.activation(T.qq[:, c:c + w], px, F.Identity, bias=MAGIC)
+            elif s == "rb":
+                wait("a", tk["ra", k])
+                ins = ac.activation(T.qq[:, c:c + w], T.qq[:, c:c + w], F.Identity, bias=-MAGIC)
+            elif s == "ym":
+                wait("v", tk["rb", k])
+                ins = ve.tensor_tensor(T.yy[:, c:c + w], px, T.qq[:, c:c + w], A.subtract)
+            elif s == "sq":
+                wait("a", tk["ym", k])
+                ins = ac.activation(px, T.yy[:, c:c + w], F.Square, bias=2047.5 + 64, scale=float(M))
+            elif s == "su":
+                wait("a", tk["sq", k])
+                ins = ac.activation(px, px, F.Identity, bias=-4096.0)
+            elif s == "za":
+                if extra is None:
+                    extra = before_za()
+                wait("v", tk["su", k], *extra)
+                ins = ve.tensor_tensor(T.zi[:, c:c + w], px, T.lt[:, c:c + w], A.max)
+            elif s == "zb":
+                wait("v", tk["za", k])
+                ins = ve.tensor_scalar(T.zj[:, c:c + w], T.zi[:, c:c + w], 7, M - 1, A.arith_shift_right, A.bitwise_and)
+            else:
+                wait("v", tk["zb", k])
+                ins = ve.tensor_copy(T.off[:, c:c + w], T.zj[:, c:c + w])
+            tk[s, k] = done(ins, name)
+        return [tk["zc", k] for k in range(len(parts))]
+
+    t_xm = []
+    for k in range(len(parts)):
+        base_mm(0, k)
+        t_xm.append(x_mm(0, k, *t_x))
+
+    def liar_tile():
+        h = COLS // 2
+        wait("p", t_lb, t_lb2)
+        wait("v", t_lc)
+        for a in range(2):
+            for s, (c5, n8, o) in enumerate(SEGS):
+                opens = s == 0 or SEGS[s - 1][0] != c5
+                closes = s == len(SEGS) - 1 or SEGS[s + 1][0] != c5
+                ins = pe.matmul(fb[a][:, c5:h:5], T.wk[:, s, :], T.lb[:, 512 * a + n8:512 * (a + 1):8], opens, closes)
+                if closes:
+                    tl = done(ins, "u%d" % (41 + a))
+            wait("v", tl)
+            tk = done(ve.tensor_tensor(T.lt[:, a * h:(a + 1) * h], fb[a][:, 0:h], T.lc[:, a * h:(a + 1) * h], A.min), "u40")
+        return [tk]
+
+    t_off = peers_from(t_xm, ORDER0, liar_tile)
+    wait("v", t_d0)
+    t_d = done(ve.memset(T.dseg[:, S - 1::S], RESET))
+    t_in16 = done(ve.tensor_scalar(T.in16[:], T.jp[:], 0.0, -1.0 / 16, A.is_equal, A.mult))
+    wait("a", t_i32)
+    t_i16 = done(ac.activation(T.i16[:], T.i32[:], F.Identity, scale=1.0 / 16), "u39")
+    t_i16 = done(ac.activation(T.ih[:], T.i32[:], F.Identity, scale=0.5), "u39")
+    wait("a", t_base0)
+    for t in (1, 2):
+        t_base[t] = done(ac.activation(bases[t][:], T.base0[:], F.Identity, bias=t * K3 / M))
+
+    ready = t_x + first
+    for t in range(RO):
+        last_round = t == RO - 1
+        groups = LAST_GROUPS if last_round else GROUPS
+        win = wins[t]
+        t_ga = []
+        for i, n in enumerate(CHUNKS):
+            n0 = starts[i]
+            src = win[:, 0:M].indirect(T.off[:, 5 * n0 // 8:5 * (n0 + n) // 8])
+            dst = T.vals[:, S * n0:S * (n0 + n)]
+            q = "v" if i == 0 else "a"
+            wait(q, t_off[part_of[i]], *ready)
+            ins = ve.tensor_copy(dst, src) if i == 0 else ac.activation(dst, src, F.Identity)
+            t_ga.append(done(ins, "ga%d" % i))
+        ready = []
+        t_xm = []
+
+        def finish(k, tok):
+            n0, n1 = starts[groups[k][0]], starts[groups[k][-1] + 1]
+            dst = T.res[:, n0:n1] if last_round else wins[t + 1][:, own + n0:own + n1]
+            wait("v", tok)
+            tf = done(ve.tensor_scalar(dst, fb[k][:, 0:n1 - n0], MAGIC, MAGIC + 17, A.add, A.subtract), "fin%d" % k)
+            if last_round:
+                wait("s", tf)
+                done(sy.dma_start(T.y[:, n0:n1], dst), "stored", 16)
+            else:
+                wait("g", tf)
+                send(dst, [(d, split[d], "arr%d" % (t + 1)) for d in peers])
+                ready.append(tf)
+                t_xm.append(x_mm(t + 1, k, tf))
+
+        pending = None
+        for k, gr in enumerate(groups):
+            for i in gr:
+                n0, n = starts[i], CHUNKS[i]
+                lo, hi = S * n0, S * (n0 + n)
+                o = n0 - starts[gr[0]]
+                acc = fb[k][:, o:o + n]
+                wait("p", t_i16, t_in16, t_ga[i])
+                pe.matmul(acc, T.ih[:], win[:, own + n0:own + n0 + n], True, False)
+                for m in range(S):
+                    pe.matmul(acc, T.i16[:], T.vals[:, lo + m:hi:S], False, False)
+                wait("v", t_d, t_ga[i])
+                done(ve.tensor_tensor_scan(T.his[:, lo:hi], T.vals[:, lo:hi], T.dseg[:, 0:S * n], 0.0, A.max, A.subtract), "sc%d" % i)
+                ts = done(ve.tensor_tensor_scan(T.los[:, lo:hi], T.dseg[:, S - 1:S - 1 + S * n], T.vals[:, lo:hi], 0.0, A.max, A.min), "sc%d" % i)
+                wait("p", ts)
+                pe.matmul(acc, T.in16[:], T.his[:, lo + S - 1:hi:S], False, False)
+                tp = done(pe.matmul(acc, T.in16[:], T.los[:, lo + S - 1:hi:S], False, True), "pe%d" % k)
+                if i == 0 and not last_round:
+                    for kk in range(len(parts)):
+                        base_mm(t + 1, kk)
+                if pending is not None:
+                    finish(*pending)
+                    pending = None
+            pending = (k, tp)
+        finish(*pending)
+        if not last_round:
+            t_off = peers_from(t_xm, ORDER, lambda: [])
+            ready.append(("arr%d" % (t + 1), landing * len(groups)))
+
+    wait("s", ("stored", count["stored"]))
+    wait("g", ("sent", count["sent"]))

@@ -3,49 +3,79 @@ from concourse.mybir import AluOpType, ActivationFunctionType
 
 V, S, M, RO = 1024, 10, 4096, 3
 K1, K2, K3, K4, K5 = 1597, 613, 911, 1223, 74
-CHUNKS = [160, 256, 192, 144, 112, 80, 48, 32]
-GROUPS = [[0, 1], [2, 3], [4, 5, 6, 7]]
-LAST_GROUPS = [[0, 1], [2, 3], [4, 5], [6, 7]]
-RELAY = 0
-NMAX = max(CHUNKS)
+NF = 224
+MV = 5
+SCAN = [("A", [144, 80]), ("B", [192, 160]), ("C", [48, 112, 64])]
+MERGE = False
+PARTS = {"P": "P", "A": "AC", "B": "B"}
+BY_VECTOR = ["A0"]
+Q_ON = {"P": "a", "A": "a", "B": "a", "C": "a"}
+Z_ON = {"P": "v", "A": "v", "B": "v", "C": "v"}
+FIN_SCALAR = "P"
+LBV = 10
+WK3 = False
+ROT = 32
+SMID = 1024
+CMID = 2040
+G = 1
+NS = S // G
+W = G * NF // 16
+KM = (K4 + K5 * CMID) % M
 MAGIC = 12582912.0
-RESET = 264.5
+RESET = 256
+WIDE = 400
 COLS = V * S // 16
-ORDER = "ra0 ra1 rb0 rb1 ym0 ym1 sq0 ra2 su0 rb2 sq1 su1 za0 ym2 zb0 za1 zc0 sq2 su2 zb1 za2 zc1 zb2 zc2".split()
-ORDER0 = "ra0 rb0 ym0 ra1 sq0 rb1 su0 ym1 ra2 sq1 rb2 su1 za0 ym2 zb0 za1 zc0 sq2 su2 zb1 za2 zc1 zb2 zc2".split()
+NMAX = max(n for _, ns in SCAN for n in ns)
+FIRST = ("bA xA qA yA TELL bB xB LIAR sA qB yB bP REST zaA zbA kP sB xP zaB qP yP zbB zcA MATE sP zcB zaP zbP zcP").split()
+ROUND = ("wrap gP fold bP+ gA0 bA+ mP gA1 gB0 oP mA0 cP cA1 bB+ cA0 hA0 mA1 eP hA1 gB1 cB0 mB0 gC0 hB0 fA mB1 cB1 mC0 cC0 hB1 fB"
+         " gC1 OWN cC1 gC2 hC0 mC1 hP xB+ cC2 fP qB+ kP+ hC1 mC2 yB+ hC2 xP+ fC sB+ qP+ xA+ yP+ zaB+ sP+ qA+ zaP+ zbP+ yA+ zbB+"
+         " sA+ zcP+ zaA+ zbA+ zcB+ zcA+").split()
 
 SCRATCH = {}
 for _names, _spec in [
-        ("w0 w1 w2", ("sbuf", [128, M], "bfloat16")),
+        ("w0 w1 w2", ("sbuf", [128, M + ROT], "bfloat16")),
         ("res lb", ("sbuf", [128, V], "bfloat16")),
         ("vals", ("sbuf", [128, V * S], "bfloat16")),
         ("his los", ("sbuf", [128, V * S], "float16")),
-        ("dseg", ("sbuf", [128, NMAX * S + 16], "float16")),
+        ("hb", ("sbuf", [128, RO, 2 * G * NF], "bfloat16")),
+        ("dtwo", ("sbuf", [128, G * NF + G], "bfloat16")),
+        ("pint", ("sbuf", [128, 144], "int32")),
+        ("sm sn", ("sbuf", [128, RO, NF], "float16")),
+        ("rp", ("sbuf", [128, NF], "bfloat16")),
+        ("dseg", ("sbuf", [128, NMAX * S + S], "bfloat16")),
         ("band", ("sbuf", [128, 8, 40], "float16")),
         ("wk", ("sbuf", [128, 12, 128], "float16")),
+        ("km", ("sbuf", [128, S, 128], "float16")),
+        ("kt", ("sbuf", [128, RO + 1, 128], "float16")),
+        ("pick", ("sbuf", [128, 144], "float16")),
+        ("ones", ("sbuf", [128, WIDE], "bfloat16")),
+        ("cf", ("sbuf", [128, W], "float16")),
+        ("lp lq", ("sbuf", [128, 2 * W], "bfloat16")),
         ("pi pj", ("sbuf", [128, 4], "int32")),
-        ("pf pc", ("sbuf", [128, 4], "float32")),
+        ("pf pc kcol", ("sbuf", [128, 8], "float32")),
         ("e5 ee a5 b5 bcol lcol", ("sbuf", [128, 8], "float32")),
         ("n8", ("sbuf", [128, 8], "int32")),
         ("m16", ("sbuf", [128, 16], "float32")),
         ("g16 kk bm", ("sbuf", [128, 8, S], "float32")),
-        ("jp i32", ("sbuf", [128, 128], "float32")),
+        ("jp", ("sbuf", [128, 144], "float32")),
+        ("i32", ("sbuf", [128, 128], "float32")),
         ("i16 ih", ("sbuf", [128, 128], "bfloat16")),
         ("in16", ("sbuf", [128, 128], "float16")),
         ("li", ("sbuf", [128, V // 16], "int32")),
         ("lf", ("sbuf", [128, V // 16], "bfloat16")),
-        ("lc lt base0 base1 base2 qq yy", ("sbuf", [128, COLS], "float32")),
+        ("ib il ld lx ly bp", ("sbuf", [128, NS * W], "float32")),
+        ("lc lt base qq", ("sbuf", [128, COLS], "float32")),
+        ("q16", ("sbuf", [128, COLS], "float16")),
         ("zi zj", ("sbuf", [128, COLS], "int32")),
         ("off", ("sbuf", [128, COLS], "uint16")),
-        ("f0 f1 f2 f3 x0 x1 x2", ("psum", [128, 512], "float32"))]:
+        ("fP fA fB fC xP xA xB sums", ("psum", [128, 512], "float32"))]:
     for _n in _names.split():
         SCRATCH[_n] = _spec
-SEMAPHORES = (["u%d" % i for i in range(48)]
-              + ["ga%d" % i for i in range(len(CHUNKS))] + ["sc%d" % i for i in range(len(CHUNKS))]
-              + ["pe%d" % i for i in range(4)] + ["fin%d" % i for i in range(4)]
-              + ["%s%d" % (a, i) for a in ("xm", "ra", "rb", "ym", "sq", "su", "za", "zb", "zc") for i in range(3)]
-              + ["hop%d" % i for i in range(4)] + ["loadx%d" % i for i in range(4)]
-              + ["arr0", "arr1", "arr2", "sent", "loadl", "stored"])
+_chunks = ["%s%d" % (k, i) for k, ns in SCAN for i in range(len(ns))]
+SEMAPHORES = (["u%d" % i for i in range(60)]
+              + [a + c for a in "gc" for c in _chunks] + ["gPv", "gPa", "xc", "ev", "wrap", "mP", "es"]
+              + [a + k for a in ("fin", "xm", "h", "r", "q", "y", "s", "za", "zb", "zc") for k in "PABC"]
+              + ["arr0", "arr1", "arr2", "tail0", "tail1", "tail2", "sent", "loadx", "loadl", "stored", "back", "liars", "near0", "near1", "near2", "loadp", "summed", "cP"])
 
 SEGS = [(c5, n8, 15 + 16 * c5 - S * n8) for c5 in range(5) for n8 in range(8) if -15 <= 16 * c5 - S * n8 <= S - 1]
 
@@ -65,6 +95,10 @@ def engine_split(src, peers, topo):
         n = len(es) // len(near)
         out[d] = es[i * n:(i + 1) * n]
     return out
+
+
+def mask_of(es):
+    return sum(1 << e for e in es)
 
 
 def rank_program(g, core, T, topo):
@@ -93,245 +127,390 @@ def rank_program(g, core, T, topo):
 
     peers = [c for c in T.cores if c != core]
     split = engine_split(core, peers, topo)
-    landing = sum(len(engine_split(c, [d for d in T.cores if d != c], topo)[core]) for c in peers)
+    lands = {c: len(engine_split(c, [d for d in T.cores if d != c], topo)[core]) for c in peers}
+    landing = sum(lands.values())
+    ender = T.cores[-1]
+    mate = [c for c in peers if c in topo.cores_of(core)][0]
+    from_mate = len(topo.engines(mate, core))
     own = rank * V
     wins = [T.w0, T.w1, T.w2]
-    bases = [T.base0, T.base1, T.base2]
-    fb = [T.f0, T.f1, T.f2, T.f3]
-    xb = [T.x0, T.x1, T.x2]
-    starts = [sum(CHUNKS[:i]) for i in range(len(CHUNKS) + 1)]
-    parts = [(starts[gr[0]], starts[gr[-1] + 1]) for gr in GROUPS]
-    part_of = {i: k for k, gr in enumerate(GROUPS) for i in gr}
+    place = own + ROT
+    there = T.rank_of(mate) * V + ROT
+    sizes = dict(SCAN)
+    y0 = NF + sum(sizes["C"])
+    spans = [{"P": (p, p + NF), "A": (y0 - p, y0 - p + NF), "C": (NF, y0), "B": (y0 + NF, V)} for p in (0, y0, 0)]
+    closing = {"%s%d" % (k, len(ns) - 1) for k, ns in SCAN}
+    part_of = {k: p for p, ks in PARTS.items() for k in ks}
+    wp = NS * W
 
-    def send(ap, plan):
+    def chunk(k, t):
+        i = int(k[1])
+        return spans[t][k[0]][0] + sum(sizes[k[0]][:i]), sizes[k[0]][i]
+
+    def send(ap, sem, near=None):
         trs = []
-        for d, es, sem in plan:
+        for d in peers:
             rid, pid = topo.addr(d, core)
-            trs.append(RemoteDMATransfer(dst_ids=[DstId(rid=rid, pnc=pid)], dma_engine_mask=sum(1 << e for e in es),
-                                         remote_sem=T.sem[sem], src=ap, dst=ap))
+            trs.append(RemoteDMATransfer(dst_ids=[DstId(rid=rid, pnc=pid)], dma_engine_mask=mask_of(split[d]),
+                                         remote_sem=T.sem[near if near and d == mate else sem], src=ap, dst=ap))
         g.remote_dma_fused(trs, local_sem=T.sem.sent)
-        count["sent"] = count.get("sent", 0) + sum(len(es) for d, es, sem in plan)
+        count["sent"] = count.get("sent", 0) + sum(len(es) for es in split.values())
 
-    pieces = max(RELAY, 1)
-    pw = V // pieces
-    t_x = [done(sy.dma_start(T.w0[:, own + j * pw:own + (j + 1) * pw], T.x[:, j * pw:(j + 1) * pw]), "loadx%d" % j, 16)
-           for j in range(pieces)]
+    def to_mate(dst, src, sem, es):
+        rid, pid = topo.addr(mate, core)
+        g.remote_dma(dst, src, T.sem[sem], T.sem.sent, pid, rid, mask_of(es))
+        count["sent"] += len(es)
+
+    def copy(q, dst, src):
+        return ve.tensor_copy(dst, src) if q == "v" else ac.activation(dst, src, F.Identity)
+
+    def band_of(s):
+        o = SEGS[s][2]
+        return T.band[:, :, o:o + 16] if WK3 else T.wk[:, s, :]
+
+    t_xp = done(sy.dma_start(T.w0[:, place:place + NF], T.x[:, 0:NF]), "loadp", 16)
+    t_x = done(sy.dma_start(T.w0[:, place + NF:place + V], T.x[:, NF:V]), "loadx", 16)
     t_l = done(ac.dma_start(T.li[:], T.liar[:]), "loadl", 16)
     fl = {"allow_small_or_imprecise_dtypes": True}
     t_pi = done(g.iota(T.pi[:, 0:1], [[0, 1]], 0, 1))
+    t_jp = done(g.iota(T.jp[:], [[1, 144]], 0, -1, **fl))
     t_e5 = done(g.iota(T.e5[:, 0:5], [[16, 5]], 0, 0, **fl))
     t_g16 = done(g.iota(T.g16[:], [[16, 8], [0, S]], 0, 0, **fl))
     t_kk = done(g.iota(T.kk[:], [[0, 8], [K5, S]], K2, 0, **fl))
-    t_jp = done(g.iota(T.jp[:], [[1, 128]], 0, -1, **fl))
-    if RELAY:
-        near = [d for d in peers if d in topo.cores_of(core)][0]
-        twin = [d for d in peers if d != near and topo.die(d) == topo.die(core)][0]
-        two = engine_split(core, [near, twin], topo)
-        first = []
-        for j in range(pieces):
-            wait("g", t_x[j])
-            send(T.w0[:, own + j * pw:own + (j + 1) * pw], [(twin, two[twin], "hop%d" % j), (near, two[near], "arr0")])
-            first.append(("hop%d" % j, len(two[twin])))
-        o2 = T.rank_of(twin) * V
-        on = topo.engines(core, near)
-        for j in range(pieces):
-            wait("g", first[j])
-            send(T.w0[:, o2 + j * pw:o2 + (j + 1) * pw], [(near, on, "arr0")])
-        first.append(("arr0", pieces * (len(two[near]) + len(on))))
-    else:
-        wait("g", t_x[0])
-        send(T.w0[:, own:own + V], [(d, split[d], "arr0") for d in peers])
-        first = [("arr0", landing)]
+    t_ib = done(g.iota(T.ib[:], [[G * KM, NS], [(16 // G * K1) % M, W]], 0, 0, **fl))
+    wait("g", t_xp)
+    send(T.w0[:, place:place + NF], "arr0", "near0")
+    wait("g", t_x)
+    send(T.w0[:, place + NF:place + V], "tail0" if core == ender else "arr0")
 
+    tk = {}
     t_z0 = done(ve.memset(T.band[:], 0.0))
-    t_d0 = done(ve.memset(T.dseg[:], 0.0))
     wait("v", t_pi)
-    ta = done(ve.tensor_scalar(T.pj[:, 0:1], T.pi[:, 0:1], 15, None, A.bitwise_and), "u47")
-    ta = done(ve.tensor_scalar(T.pj[:, 1:2], T.pi[:, 0:1], 112, None, A.bitwise_and), "u47")
+    ta = done(ve.tensor_scalar(T.pj[:, 0:1], T.pi[:, 0:1], 15, None, A.bitwise_and), "u59")
+    ta = done(ve.tensor_scalar(T.pj[:, 1:2], T.pi[:, 0:1], 112, None, A.bitwise_and), "u59")
+    ta = done(ve.tensor_scalar(T.pj[:, 2:3], T.pi[:, 0:1], 15, G - 1, A.bitwise_and, A.arith_shift_right), "u59")
+    ta = done(ve.tensor_scalar(T.pj[:, 3:4], T.pi[:, 0:1], G - 1, None, A.bitwise_and), "u59")
     step = (8 * K1) % M
-    c0 = (K1 * own) % M - 2047.5
-    tb = done(ve.tensor_scalar(T.pc[:, 0:1], T.pi[:, 0:1], step / M, c0 / M, A.mult, A.add), "u46")
-    tb = done(ve.tensor_scalar(T.pc[:, 1:2], T.pi[:, 0:1], 1024.0, float(2 ** 25 + 128 * own), A.mult, A.add), "u46")
+    big = float(2 ** 25 + 128 * place)
+    tb = done(ve.tensor_scalar(T.pc[:, 0:1], T.pi[:, 0:1], float(step), float((K1 * own) % M), A.mult, A.add), "u58")
+    tb = done(ve.tensor_scalar(T.pc[:, 1:2], T.pi[:, 0:1], 1024.0, big, A.mult, A.add), "u58")
     wait("v", ta)
-    t_pf = done(ve.tensor_copy(T.pf[:, 0:2], T.pj[:, 0:2]))
+    t_pf = done(ve.tensor_copy(T.pf[:, 0:4], T.pj[:, 0:4]))
+    wait("v", t_jp)
+    t_i32 = done(ve.tensor_scalar(T.i32[:], T.jp[:, 0:128], 0.0, None, A.is_equal))
     wait("v", t_pf, t_e5)
     t_ee = done(ve.tensor_scalar(T.ee[:, 0:5], T.e5[:, 0:5], T.pf[:, 0:1], None, A.add))
-    wait("v", t_g16)
-    t_bm = done(ve.tensor_scalar(T.bm[:], T.g16[:], T.pf[:, 1:2], 1.0 / M, A.is_equal, A.mult))
+    t_k0 = done(ve.tensor_scalar(T.pc[:, 4:5], T.pf[:, 3:4], float(K5), float(K2), A.mult, A.add))
+    t_pint = done(ve.tensor_scalar(T.pint[:], T.jp[:], T.pf[:, 0:1], 0.48 if G == 2 else 1.0, A.add, A.mult))
+    wait("v", t_k0)
+    t_kcol = done(ve.tensor_scalar(T.kcol[:, 0:5], T.e5[:, 0:5], G * K5 / 16, T.pc[:, 4:5], A.mult, A.add))
+    t_p0 = done(ve.tensor_scalar(T.pc[:, 5:6], T.pf[:, 2:3], float(K1), float((K1 * (there - ROT) + K2 * CMID) % M),
+                                 A.mult, A.add))
+    wait("v", t_pint)
+    t_pick = done(ve.tensor_scalar(T.pick[:], T.pint[:], 7.0 if G == 2 else 15.0, None, A.is_equal))
     wait("v", t_ee, tb)
     t_n8 = done(ve.tensor_scalar(T.n8[:, 0:5], T.ee[:, 0:5], -4.5, 0.1, A.add, A.mult))
-    t_a5 = done(ve.tensor_scalar(T.a5[:, 0:5], T.ee[:, 0:5], K4 / M, T.pc[:, 0:1], A.mult, A.add))
-    wait("v", t_bm, t_kk, t_z0)
-    t_band = done(ve.tensor_tensor(T.band[:, :, 15:15 + S], T.bm[:], T.kk[:], A.mult))
+    t_a5 = done(ve.tensor_scalar(T.a5[:, 0:5], T.ee[:, 0:5], float(K4), T.pc[:, 0:1], A.mult, A.add))
+    wait("v", t_p0)
+    t_pc = done(ve.tensor_scalar(T.pc[:, 2:3], T.pf[:, 3:4], float(KM), T.pc[:, 5:6], A.mult, A.add))
     wait("v", t_n8)
-    t_b5 = done(ve.tensor_scalar(T.b5[:, 0:5], T.n8[:, 0:5], (K1 - S * K4) / M, None, A.mult))
-    t_lcol = done(ve.tensor_scalar(T.lcol[:, 0:5], T.n8[:, 0:5], 128.0, T.pc[:, 1:2], A.mult, A.add))
-    wait("v", t_jp)
-    t_m16 = done(ve.tensor_scalar(T.m16[:], T.jp[:, 0:16], T.pf[:, 1:2], 0.0, A.add, A.is_equal))
+    t_b5 = done(ve.tensor_scalar(T.b5[:, 0:5], T.n8[:, 0:5], float(K1 - S * K4), None, A.mult))
+    wait("v", t_g16)
+    t_bm = done(ve.tensor_scalar(T.bm[:], T.g16[:], T.pf[:, 1:2], None, A.is_equal))
     wait("v", t_a5, t_b5)
     t_bcol = done(ve.tensor_tensor(T.bcol[:, 0:5], T.a5[:, 0:5], T.b5[:, 0:5], A.add))
-    t_i32 = done(ve.tensor_scalar(T.i32[:], T.jp[:], 0.0, None, A.is_equal))
-    wait("v", t_band)
-    for s, (c5, n8, o) in enumerate(SEGS):
-        t_wk = done(ve.tensor_copy(T.wk[:, s, :], T.band[:, :, o:o + 16]), "u45")
-    wait("v", t_l, t_m16)
-    t_lf = done(ve.tensor_scalar(T.lf[:], T.li[:], float(2 ** 30), None, A.mult))
-    wait("v", t_lcol)
-    for c5 in range(5):
-        t_lc = done(ve.tensor_scalar(T.lc[:, c5::5], T.jp[:], 1024.0, T.lcol[:, c5:c5 + 1], A.mult, A.add), "u43")
-    wait("v", t_lf)
-    for a in range(8, 16):
-        t_lb2 = done(ve.tensor_scalar(T.lb[:, 64 * a:64 * a + 64], T.lf[:], T.m16[:, a:a + 1], None, A.mult), "u37")
-
-    wait("a", t_bcol, t_jp)
-    for c5 in range(5):
-        t_base0 = done(ac.activation(T.base0[:, c5::5], T.jp[:], F.Identity, bias=T.bcol[:, c5:c5 + 1], scale=step / M), "u44")
-    wait("a", t_lf, t_m16)
-    for a in range(8):
-        t_lb = done(ac.activation(T.lb[:, 64 * a:64 * a + 64], T.lf[:], F.Identity, scale=T.m16[:, a:a + 1]), "u38")
-    t_base = [t_base0, None, None]
-
-    def base_mm(t, k):
-        n0, n1 = parts[k]
-        c, w = 5 * n0 // 8, 5 * (n1 - n0) // 8
-        wait("p", t_base[t], t_i32)
-        pe.matmul(xb[k][:, 0:w], T.i32[:], bases[t][:, c:c + w], True, False)
-
-    def x_mm(t, k, *toks):
-        n0, n1 = parts[k]
-        w = 5 * (n1 - n0) // 8
-        wait("p", t_wk, *toks)
+    wait("v", t_bm, t_kk, t_z0)
+    t_band = done(ve.tensor_tensor(T.band[:, :, 15:15 + S], T.bm[:], T.kk[:], A.mult))
+    t_m16 = done(ve.tensor_scalar(T.m16[:], T.jp[:, 0:16], T.pf[:, 1:2], 0.0, A.add, A.is_equal))
+    t_lcol = done(ve.tensor_scalar(T.lcol[:, 0:5], T.n8[:, 0:5], 128.0, T.pc[:, 1:2], A.mult, A.add))
+    t_pd = done(ve.tensor_scalar(T.pc[:, 3:4], T.pf[:, 2:3], 128.0, float(2 ** 25 + 128 * there), A.mult, A.add))
+    t_wk = t_band
+    if not WK3:
+        wait("v", t_band)
         for s, (c5, n8, o) in enumerate(SEGS):
-            ins = pe.matmul(xb[k][:, c5:w:5], T.wk[:, s, :], wins[t][:, own + n0 + n8:own + n1:8],
-                            False, s == len(SEGS) - 1)
-        return done(ins, "xm%d" % k)
+            t_wk = done(ve.tensor_copy(T.wk[:, s, :], T.band[:, :, o:o + 16]), "u56")
+    wait("v", t_l)
+    t_lf = done(ve.tensor_scalar(T.lf[:], T.li[:], float(2 ** 30), None, A.mult))
+    wait("v", t_lf, t_m16)
+    for a in range(LBV):
+        t_lb = [done(ve.tensor_scalar(T.lb[:, 64 * a:64 * a + 64], T.lf[:], T.m16[:, a:a + 1], None, A.mult), "u54")]
 
-    def peers_from(t_xm, order, before_za):
-        tk = {}
-        extra = None
-        for name in order:
-            s, k = name[:2], int(name[2])
-            c, w = 5 * parts[k][0] // 8, 5 * (parts[k][1] - parts[k][0]) // 8
-            px = xb[k][:, 0:w]
-            if s == "ra":
-                wait("a", t_xm[k])
-                ins = ac.activation(T.qq[:, c:c + w], px, F.Identity, bias=MAGIC)
-            elif s == "rb":
-                wait("a", tk["ra", k])
-                ins = ac.activation(T.qq[:, c:c + w], T.qq[:, c:c + w], F.Identity, bias=-MAGIC)
-            elif s == "ym":
-                wait("v", tk["rb", k])
-                ins = ve.tensor_tensor(T.yy[:, c:c + w], px, T.qq[:, c:c + w], A.subtract)
-            elif s == "sq":
-                wait("a", tk["ym", k])
-                ins = ac.activation(px, T.yy[:, c:c + w], F.Square, bias=2047.5 + 64, scale=float(M))
-            elif s == "su":
-                wait("a", tk["sq", k])
-                ins = ac.activation(px, px, F.Identity, bias=-4096.0)
-            elif s == "za":
-                if extra is None:
-                    extra = before_za()
-                wait("v", tk["su", k], *extra)
-                ins = ve.tensor_tensor(T.zi[:, c:c + w], px, T.lt[:, c:c + w], A.max)
-            elif s == "zb":
-                wait("v", tk["za", k])
-                ins = ve.tensor_scalar(T.zj[:, c:c + w], T.zi[:, c:c + w], 7, M - 1, A.arith_shift_right, A.bitwise_and)
-            else:
-                wait("v", tk["zb", k])
-                ins = ve.tensor_copy(T.off[:, c:c + w], T.zj[:, c:c + w])
-            tk[s, k] = done(ins, name)
-        return [tk["zc", k] for k in range(len(parts))]
+    wait("a", t_i32, t_kcol)
+    for s in range(NS):
+        t_km = done(ac.activation(T.km[:, s, :], T.i32[:], F.Identity, scale=T.kcol[:, s:s + 1] if G == 2 else float(K2 + K5 * s)), "u53")
+    wait("a", t_ib, t_pc)
+    t_baseP = done(ac.activation(T.bp[:], T.ib[:], F.Identity, bias=T.pc[:, 2:3]))
+    wait("a", t_bcol)
+    for c5 in range(5):
+        t_base = done(ac.activation(T.base[:, c5::5], T.jp[:, 0:128], F.Identity, bias=T.bcol[:, c5:c5 + 1],
+                                    scale=float(step)), "u52")
+    wait("a", t_lf, t_m16)
+    for a in range(LBV, 16):
+        ta = done(ac.activation(T.lb[:, 64 * a:64 * a + 64], T.lf[:], F.Identity, scale=T.m16[:, a:a + 1]), "u51")
+    t_lb.append(ta)
 
-    t_xm = []
-    for k in range(len(parts)):
-        base_mm(0, k)
-        t_xm.append(x_mm(0, k, *t_x))
+    def picked(out, src, n0):
+        n = 16 // G
+        for i in range(n):
+            o = 16 - G * (i + 1)
+            ins = pe.matmul(out, T.pick[:, o:o + 128], src[:, n0 + i:n0 + NF:n], i == 0, i == n - 1)
+        return ins
 
     def liar_tile():
         h = COLS // 2
-        wait("p", t_lb, t_lb2)
-        wait("v", t_lc)
-        for a in range(2):
+        wait("a", t_lcol)
+        for c5 in range(5):
+            t_lc = done(ac.activation(T.lc[:, c5::5], T.jp[:, 0:128], F.Identity, bias=T.lcol[:, c5:c5 + 1],
+                                      scale=1024.0), "u55")
+        wait("p", t_wk, *t_lb)
+        for a, bank in enumerate([T.fA, T.fB]):
             for s, (c5, n8, o) in enumerate(SEGS):
                 opens = s == 0 or SEGS[s - 1][0] != c5
                 closes = s == len(SEGS) - 1 or SEGS[s + 1][0] != c5
-                ins = pe.matmul(fb[a][:, c5:h:5], T.wk[:, s, :], T.lb[:, 512 * a + n8:512 * (a + 1):8], opens, closes)
-                if closes:
-                    tl = done(ins, "u%d" % (41 + a))
-            wait("v", tl)
-            tk = done(ve.tensor_tensor(T.lt[:, a * h:(a + 1) * h], fb[a][:, 0:h], T.lc[:, a * h:(a + 1) * h], A.min), "u40")
-        return [tk]
+                ins = pe.matmul(bank[:, c5:h:5], band_of(s), T.lb[:, a * V // 2 + n8:(a + 1) * V // 2:8], opens, closes)
+            wait("v", done(ins), t_lc)
+            tk["ltS"] = done(ve.tensor_tensor(T.lt[:, a * h:(a + 1) * h], bank[:, 0:h], T.lc[:, a * h:(a + 1) * h], A.min), "u50")
 
-    t_off = peers_from(t_xm, ORDER0, liar_tile)
-    wait("v", t_d0)
-    t_d = done(ve.memset(T.dseg[:, S - 1::S], RESET))
-    t_in16 = done(ve.tensor_scalar(T.in16[:], T.jp[:], 0.0, -1.0 / 16, A.is_equal, A.mult))
-    wait("a", t_i32)
-    t_i16 = done(ac.activation(T.i16[:], T.i32[:], F.Identity, scale=1.0 / 16), "u39")
-    t_i16 = done(ac.activation(T.ih[:], T.i32[:], F.Identity, scale=0.5), "u39")
-    wait("a", t_base0)
-    for t in (1, 2):
-        t_base[t] = done(ac.activation(bases[t][:], T.base0[:], F.Identity, bias=t * K3 / M))
+    def tell_liars():
+        wait("p", t_pick, *t_lb)
+        picked(T.fP[:, 0:W], T.lb, 0)
+        wait("a", done(picked(T.fP[:, W:2 * W], T.lb, y0)))
+        tk["lp"] = done(ac.activation(T.lp[:], T.fP[:, 0:2 * W], F.Identity))
+        wait("g", tk["lp"])
+        to_mate(T.lq[:], T.lp[:], "liars", split[mate])
+        tk["il"] = done(g.iota(T.il[:], [[0, NS], [16 // G * 128, W]], 0, 0, **fl))
+        tk["ones"] = done(g.iota(T.ones[0:32, :], [[0, WIDE]], 1, 0, **fl))
+        wait("g", done(g.iota(T.dseg[:], [[0, NMAX * S + S]], 0, 0, **fl)))
+        tk["d"] = done(g.iota(T.dseg[:, S - 1::S], [[0, NMAX + 1]], RESET, 0, **fl))
 
-    ready = t_x + first
-    for t in range(RO):
-        last_round = t == RO - 1
-        groups = LAST_GROUPS if last_round else GROUPS
+    def pairs():
+        tk["two"] = done(g.iota(T.dtwo[:], [[0, NF + 1], [RESET, G]], 0, 0, **fl))
+
+    def mate_liars():
+        wait("a", tk["il"], t_pd)
+        t1 = done(ac.activation(T.ld[:], T.il[:], F.Identity, bias=T.pc[:, 3:4]))
+        wait("p", ("liars", lands[mate]), t_km)
+        for m in range(NS):
+            ins = pe.matmul(T.fC[:, m * W:(m + 1) * W], T.km[:, m, :], T.lq[:, 0:W], True, True)
+        wait("v", t1, done(ins))
+        tk["ltP"] = done(ve.tensor_tensor(T.lx[:], T.fC[:, 0:wp], T.ld[:], A.min))
+
+    def rest():
+        for t, a in enumerate([(SMID - 7.5) / 16, K3, 2 * K3, (K3 + K1 * y0 + M // 2) % M - M // 2]):
+            tk["kt"] = done(ve.memset(T.kt[0:32, t, :], float(a)), "u48")
+        done(ac.activation(T.in16[:], T.i32[:], F.Identity, scale=-1.0 / 16), "u47")
+        done(ac.activation(T.i16[:], T.i32[:], F.Identity, scale=1.0 / 16), "u47")
+        tk["i16"] = done(ac.activation(T.ih[:], T.i32[:], F.Identity, scale=0.5), "u47")
+
+    def own_liars():
+        wait("a", tk["ltP"])
+        t1 = done(ac.activation(T.ld[:], T.ld[:], F.Identity, bias=128.0 * y0))
+        wait("p", tk["e", 0])
+        for m in range(NS):
+            ins = pe.matmul(T.sums[:, m * W:(m + 1) * W], T.km[:, m, :], T.lq[:, W:2 * W], True, True)
+        wait("v", t1, done(ins))
+        tk["lu"] = done(ve.tensor_tensor(T.ly[:], T.sums[:, 0:wp], T.ld[:], A.min))
+
+    def index_step(s, k, t):
+        n0, n1 = min(spans[t][j][0] for j in PARTS[k]), max(spans[t][j][1] for j in PARTS[k])
+        c, w = 5 * n0 // 8, 5 * (n1 - n0) // 8
+        px = T["x" + k][:, 0:w]
+        other = k == "P" and n0 > 0
+        if s == "b":
+            wait("p", t_i32, t_baseP if k == "P" else t_base)
+            if t:
+                wait("p", tk["za", k, t - 1], tk["kt"], tk["ones"])
+            pe.matmul(px, T.i32[:], T.bp[:] if k == "P" else T.base[:, c:c + w], True, False)
+            if t:
+                pe.matmul(px, T.kt[0:1, RO if other else t, :], T.ones[0:1, 0:w], False, False)
+            return
+        if s == "k":
+            wait("p", t_pick, ("near%d" % t, lands[mate]), *([tk["e", t - 1], tk["lu"]] if t else []))
+            wait("a", done(picked(T.sums[:, 0:W], wins[t], there + n0), "xc"))
+            tk["ev", t] = done(ac.activation(T.cf[:], T.sums[:, 0:W], F.Identity, bias=-float(CMID)), "ev")
+            return
+        if s == "x" and k == "P":
+            wait("p", tk["ev", t], t_km)
+            for m in range(NS):
+                ins = pe.matmul(px[:, m * W:(m + 1) * W], T.km[:, m, :], T.cf[:], False, m == NS - 1)
+        elif s == "x":
+            wait("p", t_wk, *([tk["f", "P" if j == "A" else j, t - 1] for j in PARTS[k]] if t else [t_x]))
+            for i, (c5, n8, o) in enumerate(SEGS):
+                ins = pe.matmul(T["x" + k][:, c5:w:5], band_of(i), wins[t][:, place + n0 + n8:place + n1:8],
+                                False, i == len(SEGS) - 1)
+        elif s == "q":
+            wait(Q_ON[k], tk["x", k, t], *([tk["zc", "A", t - 1]] if t and k == "P" else []))
+            ins = copy(Q_ON[k], T.zi[:, c:c + w], px)
+        elif s == "y":
+            wait("v", tk["q", k, t])
+            ins = ve.tensor_scalar(T.zj[:, c:c + w], T.zi[:, c:c + w], M - 1, None, A.bitwise_and)
+        elif s == "s":
+            wait("a", tk["y", k, t])
+            ins = ac.activation(px, T.zj[:, c:c + w], F.Square, bias=64.0)
+        elif s == "za":
+            wait("v", tk["s", k, t], tk["lu" if other else "ltP" if k == "P" else "ltS"])
+            ins = ve.tensor_tensor(T.zi[:, c:c + w], px, T.ly[:] if other else T.lx[:] if k == "P" else T.lt[:, c:c + w], A.max)
+        elif s == "zb":
+            wait("v", tk["za", k, t])
+            ins = ve.tensor_scalar(T.zj[:, c:c + w], T.zi[:, c:c + w], 7, M - 1, A.arith_shift_right, A.bitwise_and)
+        else:
+            wait(Z_ON[k], tk["zb", k, t])
+            if t:
+                wait(Z_ON[k], tk["gPa", t - 1], *[tk["gA%d" % i, t - 1] for i in range(len(sizes["A"]))])
+            ins = copy(Z_ON[k], T.off[:, c:c + w], T.zj[:, c:c + w])
+        tk[s, k, t] = done(ins, ("xm" if s == "x" else s) + k)
+
+    def gather(q, lo, hi, t, name):
+        src = wins[t][:, 0:M].indirect(T.off[:, lo // 16:hi // 16])
+        dst = T.vals[:, lo:hi]
+        wait(q, tk["zc", part_of[name[1]], t], *tk["ready", t])
+        ins = ve.tensor_copy(dst, src) if q == "v" else ac.activation(dst, src, F.Identity)
+        tk[name, t] = done(ins, name)
+
+    def round_step(s, k, t):
+        last = t == RO - 1
         win = wins[t]
-        t_ga = []
-        for i, n in enumerate(CHUNKS):
-            n0 = starts[i]
-            src = win[:, 0:M].indirect(T.off[:, 5 * n0 // 8:5 * (n0 + n) // 8])
-            dst = T.vals[:, S * n0:S * (n0 + n)]
-            q = "v" if i == 0 else "a"
-            wait(q, t_off[part_of[i]], *ready)
-            ins = ve.tensor_copy(dst, src) if i == 0 else ac.activation(dst, src, F.Identity)
-            t_ga.append(done(ins, "ga%d" % i))
-        ready = []
-        t_xm = []
-
-        def finish(k, tok):
-            n0, n1 = starts[groups[k][0]], starts[groups[k][-1] + 1]
-            dst = T.res[:, n0:n1] if last_round else wins[t + 1][:, own + n0:own + n1]
-            wait("v", tok)
-            tf = done(ve.tensor_scalar(dst, fb[k][:, 0:n1 - n0], MAGIC, MAGIC + 17, A.add, A.subtract), "fin%d" % k)
-            if last_round:
-                wait("s", tf)
-                done(sy.dma_start(T.y[:, n0:n1], dst), "stored", 16)
-            else:
-                wait("g", tf)
-                send(dst, [(d, split[d], "arr%d" % (t + 1)) for d in peers])
-                ready.append(tf)
-                t_xm.append(x_mm(t + 1, k, tf))
-
-        pending = None
-        for k, gr in enumerate(groups):
-            for i in gr:
-                n0, n = starts[i], CHUNKS[i]
-                lo, hi = S * n0, S * (n0 + n)
-                o = n0 - starts[gr[0]]
-                acc = fb[k][:, o:o + n]
-                wait("p", t_i16, t_in16, t_ga[i])
-                pe.matmul(acc, T.ih[:], win[:, own + n0:own + n0 + n], True, False)
+        grp = k[0:1]
+        span = spans[t]
+        v0 = S * span["P"][0]
+        wide = G * NF
+        if s == "wrap":
+            wait("a", tk["tail", t])
+            tk["ready", t].append(done(ac.activation(win[:, 0:ROT], win[:, M:M + ROT], F.Identity), "wrap"))
+        elif s == "g" and k == "P":
+            gather("v", v0, v0 + MV * NF, t, "gPv")
+            gather("a", v0 + MV * NF, v0 + S * NF, t, "gPa")
+        elif s == "fold":
+            wait("g", tk["gPv", t], tk["gPa", t])
+            rid, pid = topo.addr(mate, core)
+            es = topo.engines(core, mate)
+            h = len(es) // 2
+            g.remote_dma_fused([RemoteDMATransfer(
+                dst_ids=[DstId(rid=rid, pnc=pid)], dma_engine_mask=mask_of(es[h * a:h * (a + 1)]), remote_sem=T.sem.back,
+                srcs=[T.vals[:, v0 + wide * i:v0 + wide * (i + 1)] for i in range(NS)],
+                dsts=[T.hb[:, t, wide * a:wide * (a + 1)]], alu_op=2 + a) for a in range(2)], local_sem=T.sem.sent)
+            count["sent"] += len(es)
+            if t == 0 and G > 1:
+                pairs()
+        elif s == "c" and k == "P" and G == 1:
+            tk["c", k, t] = ("back", from_mate * (t + 1))
+        elif s == "c" and k == "P":
+            wait("v", tk["two"], ("back", from_mate * (t + 1)))
+            done(ve.tensor_tensor_scan(T.his[:, v0:v0 + wide], T.hb[:, t, 0:wide], T.dtwo[:, 0:wide], 0.0, A.max, A.subtract), "cP")
+            tk["c", k, t] = done(ve.tensor_tensor_scan(T.los[:, v0:v0 + wide], T.dtwo[:, G - 1:G - 1 + wide],
+                                                       T.hb[:, t, wide:2 * wide], 0.0, A.max, A.min), "cP")
+        elif s == "g":
+            n0, n = chunk(k, t)
+            gather("v" if k in BY_VECTOR else "a", S * n0, S * (n0 + n), t, "g" + k)
+        elif s == "m" and k == "P":
+            wait("p", tk["i16"], tk["gPv", t])
+            for m in range(S):
+                lo = v0 + wide * (m // G)
+                if lo + wide > v0 + MV * NF:
+                    wait("p", tk["gPa", t])
+                ins = pe.matmul(T.sums[:, 0:NF], T.i16[:], T.vals[:, lo + m % G:lo + wide:G], m == 0, m == S - 1)
+            tk["m", k, t] = done(ins, "mP")
+        elif s == "e":
+            wait("a", tk["m", k, t])
+            tk["e", t] = done(ac.activation(T.sm[:, t, :], T.sums[:, 0:NF], F.Identity, bias=-float(SMID), scale=16.0), "es")
+            wait("g", tk["e", t])
+            to_mate(T.sn[:, t, :], T.sm[:, t, :], "summed", topo.engines(core, mate))
+        elif s == "o":
+            wait("p", tk["i16"], tk["kt"], tk["ones"], tk["lp"], tk["gPv", t])
+            pe.matmul(T.fP[:, 0:NF], T.ih[:], win[:, place + span["P"][0]:place + span["P"][1]], True, False)
+            pe.matmul(T.fP[:, 0:NF], T.kt[0:1, 0, :], T.ones[0:1, 0:NF], False, False)
+        elif s == "h" and k == "P":
+            acc = T.fP[:, 0:NF]
+            wait("p", ("summed", from_mate * (t + 1)), tk["c", k, t])
+            pe.matmul(acc, T.i16[:], T.sn[:, t, :], False, False)
+            pe.matmul(acc, T.in16[:], T.his[:, v0 + G - 1:v0 + wide:G] if G > 1 else T.hb[:, t, 0:NF], False, False)
+            tk["h", k, t] = done(pe.matmul(acc, T.in16[:], T.los[:, v0 + G - 1:v0 + wide:G] if G > 1 else T.hb[:, t, NF:2 * NF],
+                                           False, True), "hP")
+        elif s in "mch":
+            n0, n = chunk(k, t)
+            lo, hi = S * n0, S * (n0 + n)
+            o = n0 - span[grp][0]
+            acc = T["f" + grp][:, o:o + n]
+            if s == "m":
+                wait("p", tk["i16"], tk["kt"], tk["ones"], tk["g" + k, t], tk["ltS"], tk["ltP"])
+                pe.matmul(acc, T.ih[:], win[:, place + n0:place + n0 + n], True, False)
+                pe.matmul(acc, T.kt[0:1, 0, :], T.ones[0:1, 0:n], False, False)
                 for m in range(S):
                     pe.matmul(acc, T.i16[:], T.vals[:, lo + m:hi:S], False, False)
-                wait("v", t_d, t_ga[i])
-                done(ve.tensor_tensor_scan(T.his[:, lo:hi], T.vals[:, lo:hi], T.dseg[:, 0:S * n], 0.0, A.max, A.subtract), "sc%d" % i)
-                ts = done(ve.tensor_tensor_scan(T.los[:, lo:hi], T.dseg[:, S - 1:S - 1 + S * n], T.vals[:, lo:hi], 0.0, A.max, A.min), "sc%d" % i)
-                wait("p", ts)
+            elif s == "c":
+                wait("v", tk["d"], tk["g" + k, t])
+                done(ve.tensor_tensor_scan(T.his[:, lo:hi], T.vals[:, lo:hi], T.dseg[:, 0:S * n], 0.0, A.max, A.subtract), "c" + k)
+                tk["c", k, t] = done(ve.tensor_tensor_scan(T.los[:, lo:hi], T.dseg[:, S - 1:S - 1 + S * n], T.vals[:, lo:hi],
+                                                           0.0, A.max, A.min), "c" + k)
+            else:
+                wait("p", tk["c", k, t])
                 pe.matmul(acc, T.in16[:], T.his[:, lo + S - 1:hi:S], False, False)
-                tp = done(pe.matmul(acc, T.in16[:], T.los[:, lo + S - 1:hi:S], False, True), "pe%d" % k)
-                if i == 0 and not last_round:
-                    for kk in range(len(parts)):
-                        base_mm(t + 1, kk)
-                if pending is not None:
-                    finish(*pending)
-                    pending = None
-            pending = (k, tp)
-        finish(*pending)
-        if not last_round:
-            t_off = peers_from(t_xm, ORDER, lambda: [])
-            ready.append(("arr%d" % (t + 1), landing * len(groups)))
+                tok = done(pe.matmul(acc, T.in16[:], T.los[:, lo + S - 1:hi:S], False, True), "h" + grp)
+                if k in closing:
+                    tk["h", grp, t] = tok
+        else:
+            n0, n1 = span[k]
+            n = n1 - n0
+            dst = wins[t + 1][:, place + n0:place + n1] if not last else T.res[:, n0:n1]
+            down = MAGIC + (RESET * (G - 1) if k == "P" else SMID + RESET) // 16
+            if k in FIN_SCALAR:
+                wait("a", tk["h", k, t])
+                wait("a", done(ac.activation(T.qq[:, 0:n], T["f" + k][:, 0:n], F.Identity, bias=MAGIC), "r" + k))
+                tf = done(ac.activation(dst, T.qq[:, 0:n], F.Identity, bias=-down), "fin" + k)
+            else:
+                wait("v", tk["h", k, t])
+                tf = done(ve.tensor_scalar(dst, T["f" + k][:, 0:n], MAGIC, down, A.add, A.subtract), "fin" + k)
+            if last:
+                wait("s", tf)
+                done(sy.dma_start(T.y[:, n0:n1], T.res[:, n0:n1]), "stored", 16)
+                return
+            tk["f", k, t] = tf
+            tk["ready", t + 1].append(tf)
+            ends = core == ender and n1 == V
+            if ends:
+                tk["tail", t + 1] = tf
+            if MERGE and k in "PC":
+                if ("f", "P", t) not in tk or ("f", "C", t) not in tk:
+                    return
+                wait("g", tk["f", "P", t], tk["f", "C", t])
+                dst = wins[t + 1][:, place + min(span["P"][0], NF):place + max(span["P"][1], y0)]
+            wait("g", tf)
+            send(dst, ("tail%d" if ends else "arr%d") % (t + 1), "near%d" % (t + 1) if k == "A" else None)
+
+    def parse(name):
+        for s in ("fold", "wrap", "za", "zb", "zc"):
+            if name.startswith(s):
+                return s, name[len(s):]
+        return name[0], name[1:]
+
+    for t in range(RO):
+        calls = 2 if t == 0 else 3 if MERGE else 4
+        tk["ready", t] = [("near%d" % t, lands[mate]), ("arr%d" % t, landing * calls - lands[mate] - lands.get(ender, 0))]
+        tk["tail", t] = ("tail%d" % t, lands[ender]) if core != ender else t_x
+    tk["ready", 0] += [t_xp, t_x]
+    for name in FIRST:
+        if name == "LIAR":
+            liar_tile()
+        elif name == "TELL":
+            tell_liars()
+        elif name == "MATE":
+            mate_liars()
+        elif name == "REST":
+            rest()
+        else:
+            index_step(*parse(name), 0)
+    for t in range(RO):
+        for name in ROUND:
+            if name == "OWN":
+                if t == 0:
+                    own_liars()
+            elif name.endswith("+"):
+                if t + 1 < RO:
+                    index_step(*parse(name[:-1]), t + 1)
+            elif name[0] in "bkxqysz":
+                index_step(*parse(name), t)
+            else:
+                round_step(*parse(name), t)
 
     wait("s", ("stored", count["stored"]))
     wait("g", ("sent", count["sent"]))

@@ -3,79 +3,82 @@ from concourse.mybir import AluOpType, ActivationFunctionType
 
 V, S, M, RO = 1024, 10, 4096, 3
 K1, K2, K3, K4, K5 = 1597, 613, 911, 1223, 74
-NF = 224
-MV = 5
-SCAN = [("A", [144, 80]), ("B", [192, 160]), ("C", [48, 112, 64])]
-MERGE = False
-PARTS = {"P": "P", "A": "AC", "B": "B"}
-BY_VECTOR = ["A0"]
-Q_ON = {"P": "a", "A": "a", "B": "a", "C": "a"}
-Z_ON = {"P": "v", "A": "v", "B": "v", "C": "v"}
-FIN_SCALAR = "P"
-LBV = 10
-WK3 = False
+GROUPS = [[("P", [224]), ("C", [96]), ("A", [128, 64]), ("D", [112, 64]), ("B", [192, 144])],
+          [("A", [128, 96]), ("C", [96]), ("P", [192]), ("D", [112, 64]), ("B", [192, 144])],
+          [("P", [224]), ("C", [64]), ("A", [144, 80]), ("D", [112, 64]), ("B", [192, 144])]]
+PARTS = [{"A": "CA", "D": "D", "B": "B"}, {"A": "AC", "D": "D", "B": "B"}, {"A": "CA", "D": "D", "B": "B"}]
+MV = [5, 5, 5]
+BY_VECTOR = [["A0"], ["A0"], ["A0"]]
+Z_ON = {"P": "v", "A": "v", "B": "a", "D": "v"}
+JOIN = ["", "", ""]
+STORE_SCALAR = "P"
+BANK = {"D": "A"}
+RELAY = ["H", "B", ""]
+HELPED = ["", "A", "AB"]
+HEAD = 448
+OPENING = [("H", "f"), ("R", "f"), ("W", "m")]
+KM_V = 5
 ROT = 32
-SMID = 1024
+SMID = 512
 CMID = 2040
-G = 1
-NS = S // G
-W = G * NF // 16
 KM = (K4 + K5 * CMID) % M
-MAGIC = 12582912.0
-RESET = 256
-WIDE = 400
+MAGIC = 12582912
+RESET = 264.5
+UP = 17
+WIDE = 512
 COLS = V * S // 16
-NMAX = max(n for _, ns in SCAN for n in ns)
-FIRST = ("bA xA qA yA TELL bB xB LIAR sA qB yB bP REST zaA zbA kP sB xP zaB qP yP zbB zcA MATE sP zcB zaP zbP zcP").split()
-ROUND = ("wrap gP fold bP+ gA0 bA+ mP gA1 gB0 oP mA0 cP cA1 bB+ cA0 hA0 mA1 eP hA1 gB1 cB0 mB0 gC0 hB0 fA mB1 cB1 mC0 cC0 hB1 fB"
-         " gC1 OWN cC1 gC2 hC0 mC1 hP xB+ cC2 fP qB+ kP+ hC1 mC2 yB+ hC2 xP+ fC sB+ qP+ xA+ yP+ zaB+ sP+ qA+ zaP+ zbP+ yA+ zbB+"
-         " sA+ zcP+ zaA+ zbA+ zcB+ zcA+").split()
+NFS = [dict(gs)["P"][0] for gs in GROUPS]
+NF = max(NFS)
+NMAX = max(n for gs in GROUPS for k, ns in gs for n in ns if k != "P")
+FIRST = ("KMa PICK BP0 KMv bP BASE WK KT kP GI xP rP dP IDv sP bB bA xB yP rB xA bD xD BP1 ROW1v rA PASS zP dA ROW0a rD sA ONES dB"
+         " sB SEG dD yB yA KEEP1a sD KEEP0v yD zB zA zD").split()
+ROUND = ("wrap gP fold gA0 bB+ gA1 bA+ oP oB oA oC mP bP+ cA1 gB0 mA0 mA1 eP cA0 mB0 hA0 gB1 gC0 hA1 cB0 hB0 mB1 mC0 fA gD0 cB1"
+         " hB1 cC0 fB gD1 hP hC0 fP xB+ kP+ mD0 mD1 fC cD0 hD0 rB+ cD1 dB+ hD1 xA+ pB sB+ fD rA+ xP+ yB+ zB+ dA+ rP+ dP+ bD+"
+         " sA+ yA+ sP+ xD+ rD+ yP+ dD+ zA+ zP+ sD+ yD+ zD+").split()
+LAST = ("wrap gP fold gA0 oP mP gA1 gB0 cA1 mA1 mA0 eP cA0 gB1 cB0 hA1 mB0 hA0 gC0 fA gD0 cB1 mB1 hB0 gD1 mC0 cC0 hB1 hC0 fB"
+        " mD0 hP fC cD0 mD1 hD0 cD1 fP hD1 fD").split()
 
 SCRATCH = {}
 for _names, _spec in [
         ("w0 w1 w2", ("sbuf", [128, M + ROT], "bfloat16")),
-        ("res lb", ("sbuf", [128, V], "bfloat16")),
+        ("res lr", ("sbuf", [128, V], "bfloat16")),
+        ("keep", ("sbuf", [128, V], "float16")),
         ("vals", ("sbuf", [128, V * S], "bfloat16")),
         ("his los", ("sbuf", [128, V * S], "float16")),
-        ("hb", ("sbuf", [128, RO, 2 * G * NF], "bfloat16")),
-        ("dtwo", ("sbuf", [128, G * NF + G], "bfloat16")),
-        ("pint", ("sbuf", [128, 144], "int32")),
+        ("hb", ("sbuf", [128, RO, 2 * NF], "bfloat16")),
         ("sm sn", ("sbuf", [128, RO, NF], "float16")),
-        ("rp", ("sbuf", [128, NF], "bfloat16")),
-        ("dseg", ("sbuf", [128, NMAX * S + S], "bfloat16")),
+        ("dseg", ("sbuf", [128, NMAX * S + S], "float16")),
         ("band", ("sbuf", [128, 8, 40], "float16")),
         ("wk", ("sbuf", [128, 12, 128], "float16")),
         ("km", ("sbuf", [128, S, 128], "float16")),
-        ("kt", ("sbuf", [128, RO + 1, 128], "float16")),
+        ("kt kp", ("sbuf", [128, RO, 128], "float16")),
         ("pick", ("sbuf", [128, 144], "float16")),
         ("ones", ("sbuf", [128, WIDE], "bfloat16")),
-        ("cf", ("sbuf", [128, W], "float16")),
-        ("lp lq", ("sbuf", [128, 2 * W], "bfloat16")),
+        ("cf", ("sbuf", [128, NF // 16], "float16")),
         ("pi pj", ("sbuf", [128, 4], "int32")),
-        ("pf pc kcol", ("sbuf", [128, 8], "float32")),
-        ("e5 ee a5 b5 bcol lcol", ("sbuf", [128, 8], "float32")),
+        ("pf pc", ("sbuf", [128, 8], "float32")),
+        ("e5 ee a5 b5 bcol", ("sbuf", [128, 8], "float32")),
         ("n8", ("sbuf", [128, 8], "int32")),
-        ("m16", ("sbuf", [128, 16], "float32")),
         ("g16 kk bm", ("sbuf", [128, 8, S], "float32")),
         ("jp", ("sbuf", [128, 144], "float32")),
-        ("i32", ("sbuf", [128, 128], "float32")),
-        ("i16 ih", ("sbuf", [128, 128], "bfloat16")),
+        ("i32 gq", ("sbuf", [128, 128], "float32")),
+        ("i16 ih gm gi dn", ("sbuf", [128, 128], "bfloat16")),
         ("in16", ("sbuf", [128, 128], "float16")),
-        ("li", ("sbuf", [128, V // 16], "int32")),
-        ("lf", ("sbuf", [128, V // 16], "bfloat16")),
-        ("ib il ld lx ly bp", ("sbuf", [128, NS * W], "float32")),
-        ("lc lt base qq", ("sbuf", [128, COLS], "float32")),
-        ("q16", ("sbuf", [128, COLS], "float16")),
+        ("li", ("sbuf", [128, V], "int32")),
+        ("ib bp", ("sbuf", [128, RO, S * NF // 16], "float32")),
+        ("base", ("sbuf", [128, COLS], "float32")),
         ("zi zj", ("sbuf", [128, COLS], "int32")),
         ("off", ("sbuf", [128, COLS], "uint16")),
+        ("mine told", ("sbuf", [128, S * NF // 16], "uint16")),
         ("fP fA fB fC xP xA xB sums", ("psum", [128, 512], "float32"))]:
     for _n in _names.split():
         SCRATCH[_n] = _spec
-_chunks = ["%s%d" % (k, i) for k, ns in SCAN for i in range(len(ns))]
+_chunks = sorted({"%s%d" % (k, i) for gs in GROUPS for k, ns in gs for i in range(len(ns)) if k != "P"})
 SEMAPHORES = (["u%d" % i for i in range(60)]
-              + [a + c for a in "gc" for c in _chunks] + ["gPv", "gPa", "xc", "ev", "wrap", "mP", "es"]
-              + [a + k for a in ("fin", "xm", "h", "r", "q", "y", "s", "za", "zb", "zc") for k in "PABC"]
-              + ["arr0", "arr1", "arr2", "tail0", "tail1", "tail2", "sent", "loadx", "loadl", "stored", "back", "liars", "near0", "near1", "near2", "loadp", "summed", "cP"])
+              + [a + c for a in "gc" for c in _chunks] + ["kmv", "kma", "idv", "ida"] + ["gPv", "gPa", "xc", "ev", "wrap", "mP", "es"]
+              + [a + k for a in ("fin", "x", "h", "r", "d", "s", "y", "z") for k in "PABD"] + ["finC", "hC"]
+              + ["arr0", "arr1", "arr2", "tail0", "tail1", "tail2", "near0", "near1", "near2", "sent", "loadx", "loadp", "loadl",
+                 "lists", "stored", "back", "summed"] + ["hand%s%d" % (k, t) for t in range(RO) for k in RELAY[t] + HELPED[t]])
 
 SEGS = [(c5, n8, 15 + 16 * c5 - S * n8) for c5 in range(5) for n8 in range(8) if -15 <= 16 * c5 - S * n8 <= S - 1]
 
@@ -101,9 +104,68 @@ def mask_of(es):
     return sum(1 << e for e in es)
 
 
+def meet(a, b):
+    return a[0] < b[1] and b[0] < a[1]
+
+
+def layout():
+    spans, chunks = [], []
+    for gs in GROUPS:
+        n, sp, ch = 0, {}, {}
+        for k, ns in gs:
+            sp[k] = (n, n + sum(ns))
+            for i, a in enumerate(ns):
+                ch["%s%d" % (k, i)] = (n, n + a)
+                n += a
+        spans.append(sp)
+        chunks.append(ch)
+    return spans, chunks
+
+
+def sem_of(src, dst, piece, t, T, topo):
+    if src == T.cores[-1] and piece[1] == V:
+        return "tail%d" % t
+    if dst in topo.cores_of(src) and meet(piece, layout()[0][t]["P"]):
+        return "near%d" % t
+    return "arr%d" % t
+
+
+def write(g, core, T, topo, moves):
+    trs = []
+    for d, es, sem, src, dst in moves:
+        rid, pid = topo.addr(d, core)
+        trs.append(RemoteDMATransfer(dst_ids=[DstId(rid=rid, pnc=pid)], dma_engine_mask=mask_of(es), remote_sem=T.sem[sem], src=src, dst=dst))
+    g.remote_dma_fused(trs, local_sem=T.sem.sent)
+    return sum(len(m[1]) for m in moves)
+
+
+def helper_of(core, T, topo):
+    return [c for c in topo.cores_of(core) if T.rank_of(c) is None and topo.die(c) == topo.die(core)][0]
+
+
+def twin_of(core, T, topo):
+    return [c for c in T.cores if c not in topo.cores_of(core) and topo.die(c) == topo.die(core)][0]
+
+
+def helper_program(g, core, T, topo):
+    src = twin_of(core, T, topo)
+    split = engine_split(core, [c for c in T.cores if c in topo.cores_of(core)], topo)
+    sent = 0
+    for t, win in ((1, T.w1), (2, T.w2)):
+        for k in HELPED[t]:
+            piece = layout()[0][t - 1][k]
+            at = T.rank_of(src) * V + ROT
+            ap = win[:, at + piece[0]:at + piece[1]]
+            g.wait_ge(T.sem["hand%s%d" % (k, t)], len(topo.engines(src, core)))
+            sent += write(g, core, T, topo, [(d, es, sem_of(src, d, piece, t, T, topo), ap, ap) for d, es in split.items()])
+    g.wait_ge(T.sem.sent, sent)
+
+
 def rank_program(g, core, T, topo):
     rank = T.rank_of(core)
     if rank is None:
+        if any(HELPED) and core in [helper_of(c, T, topo) for c in T.cores]:
+            helper_program(g, core, T, topo)
         return
     A = AluOpType
     F = ActivationFunctionType
@@ -128,7 +190,6 @@ def rank_program(g, core, T, topo):
     peers = [c for c in T.cores if c != core]
     split = engine_split(core, peers, topo)
     lands = {c: len(engine_split(c, [d for d in T.cores if d != c], topo)[core]) for c in peers}
-    landing = sum(lands.values())
     ender = T.cores[-1]
     mate = [c for c in peers if c in topo.cores_of(core)][0]
     from_mate = len(topo.engines(mate, core))
@@ -136,305 +197,323 @@ def rank_program(g, core, T, topo):
     wins = [T.w0, T.w1, T.w2]
     place = own + ROT
     there = T.rank_of(mate) * V + ROT
-    sizes = dict(SCAN)
-    y0 = NF + sum(sizes["C"])
-    spans = [{"P": (p, p + NF), "A": (y0 - p, y0 - p + NF), "C": (NF, y0), "B": (y0 + NF, V)} for p in (0, y0, 0)]
-    closing = {"%s%d" % (k, len(ns) - 1) for k, ns in SCAN}
-    part_of = {k: p for p, ks in PARTS.items() for k in ks}
-    wp = NS * W
+    spans, chunks = layout()
+    parts = [dict({p: (spans[t][ks[0]][0], spans[t][ks[-1]][1]) for p, ks in PARTS[t].items()}, P=spans[t]["P"]) for t in range(RO)]
+    units = [{k: a for k, a in sp.items() if k not in JOIN[t]} for t, sp in enumerate(spans)]
+    for t, sp in enumerate(spans):
+        units[t]["P"] = (min(sp[k][0] for k in "P" + JOIN[t]), max(sp[k][1] for k in "P" + JOIN[t]))
+    pieces = [{"H": (0, HEAD), "R": (HEAD, V), "W": (0, V)}] + units[:-1]
+    twin = twin_of(core, T, topo)
+    out = [e for d in peers if d != mate for e in split[d]]
 
-    def chunk(k, t):
-        i = int(k[1])
-        return spans[t][k[0]][0] + sum(sizes[k[0]][:i]), sizes[k[0]][i]
+    def send(k, t, to=peers):
+        piece = pieces[t][k]
+        ap = wins[t][:, place + piece[0]:place + piece[1]]
+        once = k in RELAY[t] + HELPED[t]
+        moves = [(d, split[d], sem_of(core, d, piece, t, T, topo), ap, ap) for d in to if not once or d == mate]
+        if once and twin in to:
+            moves.append((twin if k in RELAY[t] else helper_of(twin, T, topo), out, "hand%s%d" % (k, t), ap, ap))
+        issue(moves)
 
-    def send(ap, sem, near=None):
-        trs = []
-        for d in peers:
-            rid, pid = topo.addr(d, core)
-            trs.append(RemoteDMATransfer(dst_ids=[DstId(rid=rid, pnc=pid)], dma_engine_mask=mask_of(split[d]),
-                                         remote_sem=T.sem[near if near and d == mate else sem], src=ap, dst=ap))
-        g.remote_dma_fused(trs, local_sem=T.sem.sent)
-        count["sent"] = count.get("sent", 0) + sum(len(es) for es in split.values())
+    def issue(moves):
+        count["sent"] = count.get("sent", 0) + write(g, core, T, topo, moves)
 
-    def to_mate(dst, src, sem, es):
-        rid, pid = topo.addr(mate, core)
-        g.remote_dma(dst, src, T.sem[sem], T.sem.sent, pid, rid, mask_of(es))
-        count["sent"] += len(es)
+    def relay(k, t, es):
+        piece, at = pieces[t][k], T.rank_of(twin) * V + ROT
+        ap = wins[t][:, at + piece[0]:at + piece[1]]
+        wait("g", ("hand%s%d" % (k, t), len(out)))
+        return (mate, es, sem_of(twin, mate, piece, t, T, topo), ap, ap)
+
+    def sums(t, es):
+        wait("g", tk["e", t])
+        count["summed"] = count.get("summed", 0) + len(es)
+        tk["summed", t] = ("summed", count["summed"])
+        return (mate, es, "summed", T.sm[:, t, 0:NFS[t]], T.sn[:, t, 0:NFS[t]])
 
     def copy(q, dst, src):
         return ve.tensor_copy(dst, src) if q == "v" else ac.activation(dst, src, F.Identity)
 
-    def band_of(s):
-        o = SEGS[s][2]
-        return T.band[:, :, o:o + 16] if WK3 else T.wk[:, s, :]
+    def plus(q, dst, src, a):
+        return ve.tensor_scalar(dst, src, a, None, A.add) if q == "v" else ac.activation(dst, src, F.Identity, bias=a)
 
-    t_xp = done(sy.dma_start(T.w0[:, place:place + NF], T.x[:, 0:NF]), "loadp", 16)
-    t_x = done(sy.dma_start(T.w0[:, place + NF:place + V], T.x[:, NF:V]), "loadx", 16)
-    t_l = done(ac.dma_start(T.li[:], T.liar[:]), "loadl", 16)
+    tk, left = {"keep": []}, {}
+    for t in range(RO):
+        got = {}
+        tk["tail", t] = []
+        for c in peers:
+            for k, piece in pieces[t].items():
+                if t == 0 and not any(k == a and ("m" if c == mate else "f") in to for a, to in OPENING):
+                    continue
+                name, n = sem_of(c, core, piece, t, T, topo), lands[c]
+                if k in RELAY[t] and c != mate:
+                    name, n = ("hand%s%d" % (k, t), len(out)) if c == twin else (name, lands[mate])
+                if k in HELPED[t] and c != mate:
+                    n = from_mate // 2
+                got[name] = got.get(name, 0) + n
+                if c == ender and piece[1] == V:
+                    tk["tail", t] = [(name, n)]
+        tk["ready", t] = list(got.items())
+        tk["near", t] = [("near%d" % t, got["near%d" % t])] if t else []
+
+    t_xp = done(sy.dma_start(T.w0[:, place:place + HEAD], T.x[:, 0:HEAD]), "loadp", 16)
+    t_x = done(sy.dma_start(T.w0[:, place + HEAD:place + V], T.x[:, HEAD:V]), "loadx", 16)
+    t_l = done(ac.dma_start(T.li[0:8, :], T.liar[:]), "loadl", 16)
+    tk["ready", 0] += [t_xp, t_x]
+    if core == ender:
+        tk["tail", 0] = [t_x]
     fl = {"allow_small_or_imprecise_dtypes": True}
+    slot = [NFS.index(n) for n in NFS]
+
+    def fold_base(t):
+        w = NFS[t] // 16
+        return done(g.iota(T.ib[:, t, 0:S * w], [[KM, S], [(16 * K1) % M, w]], 0, 0, **fl))
+
     t_pi = done(g.iota(T.pi[:, 0:1], [[0, 1]], 0, 1))
     t_jp = done(g.iota(T.jp[:], [[1, 144]], 0, -1, **fl))
     t_e5 = done(g.iota(T.e5[:, 0:5], [[16, 5]], 0, 0, **fl))
     t_g16 = done(g.iota(T.g16[:], [[16, 8], [0, S]], 0, 0, **fl))
     t_kk = done(g.iota(T.kk[:], [[0, 8], [K5, S]], K2, 0, **fl))
-    t_ib = done(g.iota(T.ib[:], [[G * KM, NS], [(16 // G * K1) % M, W]], 0, 0, **fl))
-    wait("g", t_xp)
-    send(T.w0[:, place:place + NF], "arr0", "near0")
-    wait("g", t_x)
-    send(T.w0[:, place + NF:place + V], "tail0" if core == ender else "arr0")
+    t_ib = {0: fold_base(0)}
+    t_gq = done(g.iota(T.gq[0:8, :], [[1, 8], [0, 16]], 0, -1, **fl))
+    for k, to in OPENING:
+        wait("g", t_xp, *([] if k == "H" else [t_x]))
+        send(k, 0, [d for d in peers if ("m" if d == mate else "f") in to])
+    for t in set(slot) - {0}:
+        t_ib[t] = fold_base(t)
 
-    tk = {}
+    unit = 1.0 / M
+    step = (8 * K1) % M
     t_z0 = done(ve.memset(T.band[:], 0.0))
     wait("v", t_pi)
     ta = done(ve.tensor_scalar(T.pj[:, 0:1], T.pi[:, 0:1], 15, None, A.bitwise_and), "u59")
     ta = done(ve.tensor_scalar(T.pj[:, 1:2], T.pi[:, 0:1], 112, None, A.bitwise_and), "u59")
-    ta = done(ve.tensor_scalar(T.pj[:, 2:3], T.pi[:, 0:1], 15, G - 1, A.bitwise_and, A.arith_shift_right), "u59")
-    ta = done(ve.tensor_scalar(T.pj[:, 3:4], T.pi[:, 0:1], G - 1, None, A.bitwise_and), "u59")
-    step = (8 * K1) % M
-    big = float(2 ** 25 + 128 * place)
-    tb = done(ve.tensor_scalar(T.pc[:, 0:1], T.pi[:, 0:1], float(step), float((K1 * own) % M), A.mult, A.add), "u58")
-    tb = done(ve.tensor_scalar(T.pc[:, 1:2], T.pi[:, 0:1], 1024.0, big, A.mult, A.add), "u58")
+    tb = done(ve.tensor_scalar(T.pc[:, 0:1], T.pi[:, 0:1], step * unit, (K1 * own) % M * unit - 0.5, A.mult, A.add))
     wait("v", ta)
-    t_pf = done(ve.tensor_copy(T.pf[:, 0:4], T.pj[:, 0:4]))
+    t_pf = done(ve.tensor_copy(T.pf[:, 0:2], T.pj[:, 0:2]))
     wait("v", t_jp)
     t_i32 = done(ve.tensor_scalar(T.i32[:], T.jp[:, 0:128], 0.0, None, A.is_equal))
     wait("v", t_pf, t_e5)
     t_ee = done(ve.tensor_scalar(T.ee[:, 0:5], T.e5[:, 0:5], T.pf[:, 0:1], None, A.add))
-    t_k0 = done(ve.tensor_scalar(T.pc[:, 4:5], T.pf[:, 3:4], float(K5), float(K2), A.mult, A.add))
-    t_pint = done(ve.tensor_scalar(T.pint[:], T.jp[:], T.pf[:, 0:1], 0.48 if G == 2 else 1.0, A.add, A.mult))
-    wait("v", t_k0)
-    t_kcol = done(ve.tensor_scalar(T.kcol[:, 0:5], T.e5[:, 0:5], G * K5 / 16, T.pc[:, 4:5], A.mult, A.add))
-    t_p0 = done(ve.tensor_scalar(T.pc[:, 5:6], T.pf[:, 2:3], float(K1), float((K1 * (there - ROT) + K2 * CMID) % M),
+    t_pc = done(ve.tensor_scalar(T.pc[:, 2:3], T.pf[:, 0:1], K1 * unit, (K1 * own + K2 * CMID) % M * unit - 0.5,
                                  A.mult, A.add))
-    wait("v", t_pint)
-    t_pick = done(ve.tensor_scalar(T.pick[:], T.pint[:], 7.0 if G == 2 else 15.0, None, A.is_equal))
+    wait("v", t_g16)
+    t_bm = done(ve.tensor_scalar(T.bm[:], T.g16[:], T.pf[:, 1:2], unit, A.is_equal, A.mult))
     wait("v", t_ee, tb)
     t_n8 = done(ve.tensor_scalar(T.n8[:, 0:5], T.ee[:, 0:5], -4.5, 0.1, A.add, A.mult))
-    t_a5 = done(ve.tensor_scalar(T.a5[:, 0:5], T.ee[:, 0:5], float(K4), T.pc[:, 0:1], A.mult, A.add))
-    wait("v", t_p0)
-    t_pc = done(ve.tensor_scalar(T.pc[:, 2:3], T.pf[:, 3:4], float(KM), T.pc[:, 5:6], A.mult, A.add))
-    wait("v", t_n8)
-    t_b5 = done(ve.tensor_scalar(T.b5[:, 0:5], T.n8[:, 0:5], float(K1 - S * K4), None, A.mult))
-    wait("v", t_g16)
-    t_bm = done(ve.tensor_scalar(T.bm[:], T.g16[:], T.pf[:, 1:2], None, A.is_equal))
-    wait("v", t_a5, t_b5)
-    t_bcol = done(ve.tensor_tensor(T.bcol[:, 0:5], T.a5[:, 0:5], T.b5[:, 0:5], A.add))
+    t_a5 = done(ve.tensor_scalar(T.a5[:, 0:5], T.ee[:, 0:5], K4 * unit, T.pc[:, 0:1], A.mult, A.add))
     wait("v", t_bm, t_kk, t_z0)
     t_band = done(ve.tensor_tensor(T.band[:, :, 15:15 + S], T.bm[:], T.kk[:], A.mult))
-    t_m16 = done(ve.tensor_scalar(T.m16[:], T.jp[:, 0:16], T.pf[:, 1:2], 0.0, A.add, A.is_equal))
-    t_lcol = done(ve.tensor_scalar(T.lcol[:, 0:5], T.n8[:, 0:5], 128.0, T.pc[:, 1:2], A.mult, A.add))
-    t_pd = done(ve.tensor_scalar(T.pc[:, 3:4], T.pf[:, 2:3], 128.0, float(2 ** 25 + 128 * there), A.mult, A.add))
-    t_wk = t_band
-    if not WK3:
-        wait("v", t_band)
-        for s, (c5, n8, o) in enumerate(SEGS):
-            t_wk = done(ve.tensor_copy(T.wk[:, s, :], T.band[:, :, o:o + 16]), "u56")
-    wait("v", t_l)
-    t_lf = done(ve.tensor_scalar(T.lf[:], T.li[:], float(2 ** 30), None, A.mult))
-    wait("v", t_lf, t_m16)
-    for a in range(LBV):
-        t_lb = [done(ve.tensor_scalar(T.lb[:, 64 * a:64 * a + 64], T.lf[:], T.m16[:, a:a + 1], None, A.mult), "u54")]
+    wait("v", t_n8)
+    t_b5 = done(ve.tensor_scalar(T.b5[:, 0:5], T.n8[:, 0:5], (K1 - S * K4) * unit, None, A.mult))
+    wait("v", t_a5, t_b5)
+    t_bcol = done(ve.tensor_tensor(T.bcol[:, 0:5], T.a5[:, 0:5], T.b5[:, 0:5], A.add))
 
-    wait("a", t_i32, t_kcol)
-    for s in range(NS):
-        t_km = done(ac.activation(T.km[:, s, :], T.i32[:], F.Identity, scale=T.kcol[:, s:s + 1] if G == 2 else float(K2 + K5 * s)), "u53")
-    wait("a", t_ib, t_pc)
-    t_baseP = done(ac.activation(T.bp[:], T.ib[:], F.Identity, bias=T.pc[:, 2:3]))
-    wait("a", t_bcol)
-    for c5 in range(5):
-        t_base = done(ac.activation(T.base[:, c5::5], T.jp[:, 0:128], F.Identity, bias=T.bcol[:, c5:c5 + 1],
-                                    scale=float(step)), "u52")
-    wait("a", t_lf, t_m16)
-    for a in range(LBV, 16):
-        ta = done(ac.activation(T.lb[:, 64 * a:64 * a + 64], T.lf[:], F.Identity, scale=T.m16[:, a:a + 1]), "u51")
-    t_lb.append(ta)
+    def diagonal(q, dst, a, name):
+        wait(q, t_i32)
+        if q == "v":
+            return done(ve.tensor_scalar(dst, T.i32[:], a, None, A.mult), name + "v")
+        return done(ac.activation(dst, T.i32[:], F.Identity, scale=a), name + "a")
 
-    def picked(out, src, n0):
-        n = 16 // G
-        for i in range(n):
-            o = 16 - G * (i + 1)
-            ins = pe.matmul(out, T.pick[:, o:o + 128], src[:, n0 + i:n0 + NF:n], i == 0, i == n - 1)
-        return ins
-
-    def liar_tile():
-        h = COLS // 2
-        wait("a", t_lcol)
-        for c5 in range(5):
-            t_lc = done(ac.activation(T.lc[:, c5::5], T.jp[:, 0:128], F.Identity, bias=T.lcol[:, c5:c5 + 1],
-                                      scale=1024.0), "u55")
-        wait("p", t_wk, *t_lb)
-        for a, bank in enumerate([T.fA, T.fB]):
+    def constant(name):
+        q = name[-1]
+        if name == "WK":
+            wait("v", t_band)
             for s, (c5, n8, o) in enumerate(SEGS):
-                opens = s == 0 or SEGS[s - 1][0] != c5
-                closes = s == len(SEGS) - 1 or SEGS[s + 1][0] != c5
-                ins = pe.matmul(bank[:, c5:h:5], band_of(s), T.lb[:, a * V // 2 + n8:(a + 1) * V // 2:8], opens, closes)
-            wait("v", done(ins), t_lc)
-            tk["ltS"] = done(ve.tensor_tensor(T.lt[:, a * h:(a + 1) * h], bank[:, 0:h], T.lc[:, a * h:(a + 1) * h], A.min), "u50")
-
-    def tell_liars():
-        wait("p", t_pick, *t_lb)
-        picked(T.fP[:, 0:W], T.lb, 0)
-        wait("a", done(picked(T.fP[:, W:2 * W], T.lb, y0)))
-        tk["lp"] = done(ac.activation(T.lp[:], T.fP[:, 0:2 * W], F.Identity))
-        wait("g", tk["lp"])
-        to_mate(T.lq[:], T.lp[:], "liars", split[mate])
-        tk["il"] = done(g.iota(T.il[:], [[0, NS], [16 // G * 128, W]], 0, 0, **fl))
-        tk["ones"] = done(g.iota(T.ones[0:32, :], [[0, WIDE]], 1, 0, **fl))
-        wait("g", done(g.iota(T.dseg[:], [[0, NMAX * S + S]], 0, 0, **fl)))
-        tk["d"] = done(g.iota(T.dseg[:, S - 1::S], [[0, NMAX + 1]], RESET, 0, **fl))
-
-    def pairs():
-        tk["two"] = done(g.iota(T.dtwo[:], [[0, NF + 1], [RESET, G]], 0, 0, **fl))
-
-    def mate_liars():
-        wait("a", tk["il"], t_pd)
-        t1 = done(ac.activation(T.ld[:], T.il[:], F.Identity, bias=T.pc[:, 3:4]))
-        wait("p", ("liars", lands[mate]), t_km)
-        for m in range(NS):
-            ins = pe.matmul(T.fC[:, m * W:(m + 1) * W], T.km[:, m, :], T.lq[:, 0:W], True, True)
-        wait("v", t1, done(ins))
-        tk["ltP"] = done(ve.tensor_tensor(T.lx[:], T.fC[:, 0:wp], T.ld[:], A.min))
-
-    def rest():
-        for t, a in enumerate([(SMID - 7.5) / 16, K3, 2 * K3, (K3 + K1 * y0 + M // 2) % M - M // 2]):
-            tk["kt"] = done(ve.memset(T.kt[0:32, t, :], float(a)), "u48")
-        done(ac.activation(T.in16[:], T.i32[:], F.Identity, scale=-1.0 / 16), "u47")
-        done(ac.activation(T.i16[:], T.i32[:], F.Identity, scale=1.0 / 16), "u47")
-        tk["i16"] = done(ac.activation(T.ih[:], T.i32[:], F.Identity, scale=0.5), "u47")
-
-    def own_liars():
-        wait("a", tk["ltP"])
-        t1 = done(ac.activation(T.ld[:], T.ld[:], F.Identity, bias=128.0 * y0))
-        wait("p", tk["e", 0])
-        for m in range(NS):
-            ins = pe.matmul(T.sums[:, m * W:(m + 1) * W], T.km[:, m, :], T.lq[:, W:2 * W], True, True)
-        wait("v", t1, done(ins))
-        tk["lu"] = done(ve.tensor_tensor(T.ly[:], T.sums[:, 0:wp], T.ld[:], A.min))
+                tk["wk"] = done(ve.tensor_copy(T.wk[:, s, :], T.band[:, :, o:o + 16]), "u56")
+        elif name == "PICK":
+            tk["pick"] = done(ve.tensor_scalar(T.pick[:], T.jp[:], T.pf[:, 0:1], 15.0, A.add, A.is_equal))
+        elif name[:3] == "ROW":
+            a = slice(int(name[3]) * V // 2, (int(name[3]) + 1) * V // 2)
+            wait(q, t_l)
+            tk["row", name[3]] = done(plus(q, T.lr[0:8, a], T.li[0:8, a], 1.0))
+        elif name[:2] == "KM":
+            for m in range(KM_V) if q == "v" else range(KM_V, S):
+                tk["km" + q] = diagonal(q, T.km[:, m, :], (K2 + K5 * m) * unit, "km")
+        elif name == "BASE":
+            wait("a", t_bcol)
+            for c5 in range(5):
+                tk["base"] = done(ac.activation(T.base[:, c5::5], T.jp[:, 0:128], F.Identity, bias=T.bcol[:, c5:c5 + 1],
+                                                scale=step * unit), "u52")
+        elif name[:2] == "BP":
+            t = int(q)
+            w = S * NFS[t] // 16
+            wait("a", t_ib[t], t_pc)
+            tk["bp", t] = done(ac.activation(T.bp[:, t, 0:w], T.ib[:, t, 0:w], F.Identity, bias=T.pc[:, 2:3], scale=unit))
+        elif name == "KT":
+            done(ve.memset(T.kt[0:1, 0, :], (SMID - 7.5) / 16 + UP), "u48")
+            for t in range(1, RO):
+                done(ve.memset(T.kt[0:1, t, :], K3 * t * unit), "u48")
+                tk["kt"] = done(ve.memset(T.kp[0:1, t, :], ((K3 * t + K1 * (there - place + spans[t]["P"][0]) + M // 2) % M - M // 2) * unit),
+                                "u48")
+        elif name == "PASS":
+            if "H" in RELAY[0]:
+                issue([relay("H", 0, split[mate])])
+        elif name == "ONES":
+            done(g.iota(T.dn[0:2, :], [[0, 128]], -MAGIC, MAGIC - UP, **fl), "u58")
+            tk["ones"] = done(g.iota(T.ones[0:2, :], [[0, WIDE]], 1, 0, **fl), "u58")
+        elif name == "GI":
+            wait("v", t_gq)
+            for buf, a in ((T.gi, -256.0), (T.gm, float(MAGIC))):
+                tk["gi"] = done(ve.tensor_scalar(buf[0:8, :], T.gq[0:8, :], 0.0, a, A.is_equal, A.mult), "u49")
+        elif name == "SEG":
+            wait("v", done(ve.memset(T.dseg[:], 0.0)))
+            tk["d"] = done(ve.memset(T.dseg[:, S - 1::S], RESET))
+        elif name[:2] == "ID":
+            for buf, a in ((T.ih, 0.5), (T.in16, -1.0 / 16), (T.i16, 1.0 / 16)):
+                tk["i16"] = diagonal(q, buf[:], a, "id")
+        else:
+            a = int(name[4])
+            n0, n1 = a * V // 2, (a + 1) * V // 2
+            bank, x = [T.fA, T.fB][a][:], T.w0[:, place + n0:place + n1]
+            wait("p", tk["gi"], tk["row", name[4]], tk["i16"], t_xp, t_x)
+            pe.matmul(bank, T.ih[:], x, True, False)
+            pe.matmul(bank, T.ih[:], x, False, False)
+            wait(q, done(pe.matmul(bank, T.gi[0:8, :], T.lr[0:8, n0:n1], False, True)))
+            tk["keep"].append(done(plus(q, T.keep[:, n0:n1], bank, 512.0)))
 
     def index_step(s, k, t):
-        n0, n1 = min(spans[t][j][0] for j in PARTS[k]), max(spans[t][j][1] for j in PARTS[k])
+        n0, n1 = parts[t][k]
         c, w = 5 * n0 // 8, 5 * (n1 - n0) // 8
-        px = T["x" + k][:, 0:w]
-        other = k == "P" and n0 > 0
+        bank = T.sums if k == "D" else T["x" + k]
+        px = bank[:, 0:w]
+        wp = w // S
         if s == "b":
-            wait("p", t_i32, t_baseP if k == "P" else t_base)
+            wait("p", t_i32, tk["bp", slot[t]] if k == "P" else tk["base"])
+            if k == "D":
+                wait("p", tk["ev", t])
             if t:
-                wait("p", tk["za", k, t - 1], tk["kt"], tk["ones"])
-            pe.matmul(px, T.i32[:], T.bp[:] if k == "P" else T.base[:, c:c + w], True, False)
+                wait("p", tk["r", k, t - 1], tk["kt"], tk["ones"])
+            pe.matmul(px, T.i32[:], T.bp[:, slot[t], 0:w] if k == "P" else T.base[:, c:c + w], True, False)
             if t:
-                pe.matmul(px, T.kt[0:1, RO if other else t, :], T.ones[0:1, 0:w], False, False)
+                pe.matmul(px, (T.kp if k == "P" else T.kt)[0:1, t, :], T.ones[0:1, 0:w], False, False)
             return
         if s == "k":
-            wait("p", t_pick, ("near%d" % t, lands[mate]), *([tk["e", t - 1], tk["lu"]] if t else []))
-            wait("a", done(picked(T.sums[:, 0:W], wins[t], there + n0), "xc"))
-            tk["ev", t] = done(ac.activation(T.cf[:], T.sums[:, 0:W], F.Identity, bias=-float(CMID)), "ev")
+            wait("p", tk["pick"], *tk["near", t], *([tk["e", t - 1]] if t else [t_xp] if n1 <= HEAD else [t_xp, t_x]))
+            at = there if t else place
+            for i in range(16):
+                ins = pe.matmul(T.sums[:, 0:wp], T.pick[:, 15 - i:143 - i], wins[t][:, at + n0 + i:at + n1:16], i == 0, i == 15)
+            wait("a", done(ins, "xc"))
+            tk["ev", t] = done(ac.activation(T.cf[:, 0:wp], T.sums[:, 0:wp], F.Identity, bias=-float(CMID)), "ev")
             return
         if s == "x" and k == "P":
-            wait("p", tk["ev", t], t_km)
-            for m in range(NS):
-                ins = pe.matmul(px[:, m * W:(m + 1) * W], T.km[:, m, :], T.cf[:], False, m == NS - 1)
+            wait("p", tk["ev", t], tk["kmv"], tk["kma"])
+            for m in range(S):
+                ins = pe.matmul(px[:, m * wp:(m + 1) * wp], T.km[:, m, :], T.cf[:, 0:wp], False, m == S - 1)
         elif s == "x":
-            wait("p", t_wk, *([tk["f", "P" if j == "A" else j, t - 1] for j in PARTS[k]] if t else [t_x]))
+            wait("p", tk["wk"], *([tk["f", j, t - 1] for j, a in units[t - 1].items() if meet(a, (n0, n1))] if t else [t_xp, t_x]))
             for i, (c5, n8, o) in enumerate(SEGS):
-                ins = pe.matmul(T["x" + k][:, c5:w:5], band_of(i), wins[t][:, place + n0 + n8:place + n1:8],
+                ins = pe.matmul(bank[:, c5:w:5], T.wk[:, i, :], wins[t][:, place + n0 + n8:place + n1:8],
                                 False, i == len(SEGS) - 1)
-        elif s == "q":
-            wait(Q_ON[k], tk["x", k, t], *([tk["zc", "A", t - 1]] if t and k == "P" else []))
-            ins = copy(Q_ON[k], T.zi[:, c:c + w], px)
-        elif s == "y":
-            wait("v", tk["q", k, t])
+        elif s == "r":
+            wait("a", tk["x", k, t])
+            ins = ac.activation(T.zi[:, c:c + w], px, F.Identity, bias=M / 2, scale=float(M))
+        elif s == "d":
+            wait("v", tk["r", k, t])
             ins = ve.tensor_scalar(T.zj[:, c:c + w], T.zi[:, c:c + w], M - 1, None, A.bitwise_and)
         elif s == "s":
-            wait("a", tk["y", k, t])
-            ins = ac.activation(px, T.zj[:, c:c + w], F.Square, bias=64.0)
-        elif s == "za":
-            wait("v", tk["s", k, t], tk["lu" if other else "ltP" if k == "P" else "ltS"])
-            ins = ve.tensor_tensor(T.zi[:, c:c + w], px, T.ly[:] if other else T.lx[:] if k == "P" else T.lt[:, c:c + w], A.max)
-        elif s == "zb":
-            wait("v", tk["za", k, t])
+            wait("a", tk["d", k, t])
+            ins = ac.activation(T.zi[:, c:c + w], T.zj[:, c:c + w], F.Square, bias=64.0)
+        elif s == "y":
+            wait("v", tk["s", k, t])
             ins = ve.tensor_scalar(T.zj[:, c:c + w], T.zi[:, c:c + w], 7, M - 1, A.arith_shift_right, A.bitwise_and)
         else:
-            wait(Z_ON[k], tk["zb", k, t])
+            wait(Z_ON[k], tk["y", k, t])
             if t:
-                wait(Z_ON[k], tk["gPa", t - 1], *[tk["gA%d" % i, t - 1] for i in range(len(sizes["A"]))])
-            ins = copy(Z_ON[k], T.off[:, c:c + w], T.zj[:, c:c + w])
-        tk[s, k, t] = done(ins, ("xm" if s == "x" else s) + k)
+                for j, a in chunks[t - 1].items():
+                    if meet(a, (n0, n1)):
+                        wait(Z_ON[k], *([tk["gPa", t - 1], tk["gPv", t - 1]] if j == "P0" else [tk["g" + j, t - 1]]))
+            ins = copy(Z_ON[k], (T.off if t or k != "P" else T.mine)[:, c:c + w], T.zj[:, c:c + w])
+        tk[s, k, t] = done(ins, s + k)
+        if (s, k, t) == ("z", "P", 0):
+            wait("g", tk[s, k, t])
+            issue([(mate, split[mate], "lists", T.mine[:, c:c + w], T.told[:, c:c + w])])
+            tk[s, k, t] = ("lists", lands[mate])
 
     def gather(q, lo, hi, t, name):
-        src = wins[t][:, 0:M].indirect(T.off[:, lo // 16:hi // 16])
+        src = wins[t][:, 0:M].indirect((T.off if t or name[1] != "P" else T.told)[:, lo // 16:hi // 16])
         dst = T.vals[:, lo:hi]
-        wait(q, tk["zc", part_of[name[1]], t], *tk["ready", t])
-        ins = ve.tensor_copy(dst, src) if q == "v" else ac.activation(dst, src, F.Identity)
-        tk[name, t] = done(ins, name)
+        wait(q, *[tk["z", p, t] for p, a in parts[t].items() if meet(a, (lo // S, hi // S))], *tk["ready", t])
+        tk[name, t] = done(copy(q, dst, src), name)
 
     def round_step(s, k, t):
         last = t == RO - 1
         win = wins[t]
         grp = k[0:1]
         span = spans[t]
-        v0 = S * span["P"][0]
-        wide = G * NF
-        if s == "wrap":
-            wait("a", tk["tail", t])
+        p0, nf, mv = span["P"][0], NFS[t], MV[t]
+        v0 = S * p0
+
+        def close(acc, n0, n, name, stop=True):
+            pe.matmul(acc, T.gm[0:8, :], T.lr[0:8, n0:n0 + n], False, False)
+            return done(pe.matmul(acc, T.dn[0:2, :], T.ones[0:2, 0:n], False, stop), name)
+
+        if s == "p":
+            if k in RELAY[t + 1]:
+                issue([relay(k, t + 1, split[mate])])
+        elif s == "wrap":
+            wait("a", *tk["tail", t])
             tk["ready", t].append(done(ac.activation(win[:, 0:ROT], win[:, M:M + ROT], F.Identity), "wrap"))
         elif s == "g" and k == "P":
-            gather("v", v0, v0 + MV * NF, t, "gPv")
-            gather("a", v0 + MV * NF, v0 + S * NF, t, "gPa")
+            gather("v", v0, v0 + mv * nf, t, "gPv")
+            gather("a", v0 + mv * nf, v0 + S * nf, t, "gPa")
         elif s == "fold":
             wait("g", tk["gPv", t], tk["gPa", t])
             rid, pid = topo.addr(mate, core)
             es = topo.engines(core, mate)
-            h = len(es) // 2
+            ops = [int(k)] if k else [0, 1]
+            h = len(es) // len(ops)
             g.remote_dma_fused([RemoteDMATransfer(
-                dst_ids=[DstId(rid=rid, pnc=pid)], dma_engine_mask=mask_of(es[h * a:h * (a + 1)]), remote_sem=T.sem.back,
-                srcs=[T.vals[:, v0 + wide * i:v0 + wide * (i + 1)] for i in range(NS)],
-                dsts=[T.hb[:, t, wide * a:wide * (a + 1)]], alu_op=2 + a) for a in range(2)], local_sem=T.sem.sent)
+                dst_ids=[DstId(rid=rid, pnc=pid)], dma_engine_mask=mask_of(es[h * j:h * (j + 1)]), remote_sem=T.sem.back,
+                srcs=[T.vals[:, v0 + nf * i:v0 + nf * (i + 1)] for i in range(S)],
+                dsts=[T.hb[:, t, nf * a:nf * (a + 1)]], alu_op=2 + a) for j, a in enumerate(ops)], local_sem=T.sem.sent)
             count["sent"] += len(es)
-            if t == 0 and G > 1:
-                pairs()
-        elif s == "c" and k == "P" and G == 1:
-            tk["c", k, t] = ("back", from_mate * (t + 1))
-        elif s == "c" and k == "P":
-            wait("v", tk["two"], ("back", from_mate * (t + 1)))
-            done(ve.tensor_tensor_scan(T.his[:, v0:v0 + wide], T.hb[:, t, 0:wide], T.dtwo[:, 0:wide], 0.0, A.max, A.subtract), "cP")
-            tk["c", k, t] = done(ve.tensor_tensor_scan(T.los[:, v0:v0 + wide], T.dtwo[:, G - 1:G - 1 + wide],
-                                                       T.hb[:, t, wide:2 * wide], 0.0, A.max, A.min), "cP")
+            count["back"] = count.get("back", 0) + from_mate
         elif s == "g":
-            n0, n = chunk(k, t)
-            gather("v" if k in BY_VECTOR else "a", S * n0, S * (n0 + n), t, "g" + k)
+            n0, n1 = chunks[t][k]
+            gather("v" if k in BY_VECTOR[t] else "a", S * n0, S * n1, t, "g" + k)
         elif s == "m" and k == "P":
-            wait("p", tk["i16"], tk["gPv", t])
+            wait("p", tk["i16"], tk["gPv", t], *([tk["r", "D", t]] if "D" in parts[t] else []))
             for m in range(S):
-                lo = v0 + wide * (m // G)
-                if lo + wide > v0 + MV * NF:
+                if m >= mv:
                     wait("p", tk["gPa", t])
-                ins = pe.matmul(T.sums[:, 0:NF], T.i16[:], T.vals[:, lo + m % G:lo + wide:G], m == 0, m == S - 1)
+                ins = pe.matmul(T.sums[:, 0:nf], T.i16[:], T.vals[:, v0 + nf * m:v0 + nf * (m + 1)], m == 0, m == S - 1)
             tk["m", k, t] = done(ins, "mP")
         elif s == "e":
             wait("a", tk["m", k, t])
-            tk["e", t] = done(ac.activation(T.sm[:, t, :], T.sums[:, 0:NF], F.Identity, bias=-float(SMID), scale=16.0), "es")
-            wait("g", tk["e", t])
-            to_mate(T.sn[:, t, :], T.sm[:, t, :], "summed", topo.engines(core, mate))
+            tk["e", t] = done(ac.activation(T.sm[:, t, 0:nf], T.sums[:, 0:nf], F.Identity, bias=-float(SMID), scale=16.0), "es")
+            issue([sums(t, topo.engines(core, mate))])
         elif s == "o":
-            wait("p", tk["i16"], tk["kt"], tk["ones"], tk["lp"], tk["gPv", t])
-            pe.matmul(T.fP[:, 0:NF], T.ih[:], win[:, place + span["P"][0]:place + span["P"][1]], True, False)
-            pe.matmul(T.fP[:, 0:NF], T.kt[0:1, 0, :], T.ones[0:1, 0:NF], False, False)
+            a, b = units[t][k]
+            acc = T["f" + BANK.get(k, k)][:, 0:b - a]
+            wait("p", tk["i16"], *tk["keep"], *([tk["f", j, t - 1] for j in units[t - 1]] if t else []))
+            if k in BANK:
+                wait("p", tk["f", BANK[k], t])
+            left[k, t] = sum(meet(c, (a, b)) for c in chunks[t].values())
+            pe.matmul(acc, T.ih[:], win[:, place + a:place + b], True, False)
+            if k == "P":
+                wait("p", tk["kt"], tk["ones"])
+                pe.matmul(acc[:, p0 - a:p0 - a + nf], T.kt[0:1, 0, :], T.ones[0:1, 0:nf], False, False)
         elif s == "h" and k == "P":
-            acc = T.fP[:, 0:NF]
-            wait("p", ("summed", from_mate * (t + 1)), tk["c", k, t])
-            pe.matmul(acc, T.i16[:], T.sn[:, t, :], False, False)
-            pe.matmul(acc, T.in16[:], T.his[:, v0 + G - 1:v0 + wide:G] if G > 1 else T.hb[:, t, 0:NF], False, False)
-            tk["h", k, t] = done(pe.matmul(acc, T.in16[:], T.los[:, v0 + G - 1:v0 + wide:G] if G > 1 else T.hb[:, t, NF:2 * NF],
-                                           False, True), "hP")
+            o = p0 - units[t]["P"][0]
+            acc = T.fP[:, o:o + nf]
+            wait("p", tk["summed", t], ("back", count["back"]))
+            pe.matmul(acc, T.i16[:], T.sn[:, t, 0:nf], False, False)
+            pe.matmul(acc, T.in16[:], T.hb[:, t, 0:nf], False, False)
+            pe.matmul(acc, T.in16[:], T.hb[:, t, nf:2 * nf], False, False)
+            left[k, t] -= 1
+            tk["h", k, t] = close(acc, p0, nf, "hP", left[k, t] == 0)
         elif s in "mch":
-            n0, n = chunk(k, t)
-            lo, hi = S * n0, S * (n0 + n)
-            o = n0 - span[grp][0]
-            acc = T["f" + grp][:, o:o + n]
+            n0, n1 = chunks[t][k]
+            n = n1 - n0
+            lo, hi = S * n0, S * n1
+            if grp in JOIN[t]:
+                grp = "P"
+            o = n0 - units[t][grp][0]
+            acc = T["f" + BANK.get(grp, grp)][:, o:o + n]
             if s == "m":
-                wait("p", tk["i16"], tk["kt"], tk["ones"], tk["g" + k, t], tk["ltS"], tk["ltP"])
-                pe.matmul(acc, T.ih[:], win[:, place + n0:place + n0 + n], True, False)
-                pe.matmul(acc, T.kt[0:1, 0, :], T.ones[0:1, 0:n], False, False)
+                if (grp, t) not in left:
+                    round_step("o", grp, t)
+                wait("p", tk["g" + k, t])
                 for m in range(S):
                     pe.matmul(acc, T.i16[:], T.vals[:, lo + m:hi:S], False, False)
             elif s == "c":
@@ -443,72 +522,44 @@ def rank_program(g, core, T, topo):
                 tk["c", k, t] = done(ve.tensor_tensor_scan(T.los[:, lo:hi], T.dseg[:, S - 1:S - 1 + S * n], T.vals[:, lo:hi],
                                                            0.0, A.max, A.min), "c" + k)
             else:
-                wait("p", tk["c", k, t])
+                wait("p", tk["c", k, t], tk["kt"], tk["ones"])
                 pe.matmul(acc, T.in16[:], T.his[:, lo + S - 1:hi:S], False, False)
-                tok = done(pe.matmul(acc, T.in16[:], T.los[:, lo + S - 1:hi:S], False, True), "h" + grp)
-                if k in closing:
-                    tk["h", grp, t] = tok
+                pe.matmul(acc, T.in16[:], T.los[:, lo + S - 1:hi:S], False, False)
+                left[grp, t] -= 1
+                tk["h", grp, t] = close(acc, n0, n, "h" + grp, left[grp, t] == 0)
         else:
-            n0, n1 = span[k]
-            n = n1 - n0
+            n0, n1 = units[t][k]
+            assert left[k, t] == 0
             dst = wins[t + 1][:, place + n0:place + n1] if not last else T.res[:, n0:n1]
-            down = MAGIC + (RESET * (G - 1) if k == "P" else SMID + RESET) // 16
-            if k in FIN_SCALAR:
-                wait("a", tk["h", k, t])
-                wait("a", done(ac.activation(T.qq[:, 0:n], T["f" + k][:, 0:n], F.Identity, bias=MAGIC), "r" + k))
-                tf = done(ac.activation(dst, T.qq[:, 0:n], F.Identity, bias=-down), "fin" + k)
-            else:
-                wait("v", tk["h", k, t])
-                tf = done(ve.tensor_scalar(dst, T["f" + k][:, 0:n], MAGIC, down, A.add, A.subtract), "fin" + k)
-            if last:
-                wait("s", tf)
-                done(sy.dma_start(T.y[:, n0:n1], T.res[:, n0:n1]), "stored", 16)
-                return
+            wait("v", tk["h", k, t])
+            tf = done(ve.tensor_tensor(dst, T["f" + BANK.get(k, k)][:, 0:n1 - n0], T.keep[:, n0:n1], A.min), "fin" + k)
             tk["f", k, t] = tf
+            if last:
+                q = "a" if k in STORE_SCALAR else "s"
+                wait(q, tf)
+                done(queues[q].dma_start(T.y[:, n0:n1], T.res[:, n0:n1]), "stored", 16)
+                return
             tk["ready", t + 1].append(tf)
-            ends = core == ender and n1 == V
-            if ends:
-                tk["tail", t + 1] = tf
-            if MERGE and k in "PC":
-                if ("f", "P", t) not in tk or ("f", "C", t) not in tk:
-                    return
-                wait("g", tk["f", "P", t], tk["f", "C", t])
-                dst = wins[t + 1][:, place + min(span["P"][0], NF):place + max(span["P"][1], y0)]
+            if core == ender and n1 == V:
+                tk["tail", t + 1] = [tf]
             wait("g", tf)
-            send(dst, ("tail%d" if ends else "arr%d") % (t + 1), "near%d" % (t + 1) if k == "A" else None)
+            send(k, t + 1)
 
     def parse(name):
-        for s in ("fold", "wrap", "za", "zb", "zc"):
+        for s in ("fold", "wrap"):
             if name.startswith(s):
                 return s, name[len(s):]
         return name[0], name[1:]
 
-    for t in range(RO):
-        calls = 2 if t == 0 else 3 if MERGE else 4
-        tk["ready", t] = [("near%d" % t, lands[mate]), ("arr%d" % t, landing * calls - lands[mate] - lands.get(ender, 0))]
-        tk["tail", t] = ("tail%d" % t, lands[ender]) if core != ender else t_x
-    tk["ready", 0] += [t_xp, t_x]
     for name in FIRST:
-        if name == "LIAR":
-            liar_tile()
-        elif name == "TELL":
-            tell_liars()
-        elif name == "MATE":
-            mate_liars()
-        elif name == "REST":
-            rest()
+        if name[0].isupper():
+            constant(name)
         else:
             index_step(*parse(name), 0)
     for t in range(RO):
-        for name in ROUND:
-            if name == "OWN":
-                if t == 0:
-                    own_liars()
-            elif name.endswith("+"):
-                if t + 1 < RO:
-                    index_step(*parse(name[:-1]), t + 1)
-            elif name[0] in "bkxqysz":
-                index_step(*parse(name), t)
+        for name in ROUND if t + 1 < RO else LAST:
+            if name.endswith("+"):
+                index_step(*parse(name[:-1]), t + 1)
             else:
                 round_step(*parse(name), t)
 

from concourse.bass import DstId, RemoteDMATransfer
from concourse.mybir import AluOpType, ActivationFunctionType

V, S, M, RO = 1024, 10, 4096, 3
K1, K2, K3, K4, K5 = 1597, 613, 911, 1223, 74
GROUPS = [[("P", [224]), ("C", [96]), ("A", [128, 64]), ("D", [112, 64]), ("B", [192, 144])],
          [("A", [128, 96]), ("C", [96]), ("P", [192]), ("D", [112, 64]), ("B", [192, 144])],
          [("P", [224]), ("C", [64]), ("A", [144, 80]), ("D", [112, 64]), ("B", [192, 144])]]
PARTS = [{"A": "CA", "D": "D", "B": "B"}, {"A": "AC", "D": "D", "B": "B"}, {"A": "CA", "D": "D", "B": "B"}]
MV = [5, 5, 5]
BY_VECTOR = [["A0"], ["A0"], ["A0"]]
Z_ON = {"P": "v", "A": "v", "B": "a", "D": "v"}
JOIN = ["", "", ""]
STORE_SCALAR = "P"
BANK = {"D": "A"}
RELAY = ["H", "B", ""]
HELPED = ["", "A", "AB"]
HEAD = 448
OPENING = [("H", "f"), ("R", "f"), ("W", "m")]
KM_V = 5
ROT = 32
SMID = 512
CMID = 2040
KM = (K4 + K5 * CMID) % M
MAGIC = 12582912
RESET = 264.5
UP = 17
WIDE = 512
COLS = V * S // 16
NFS = [dict(gs)["P"][0] for gs in GROUPS]
NF = max(NFS)
NMAX = max(n for gs in GROUPS for k, ns in gs for n in ns if k != "P")
FIRST = ("KMa PICK BP0 KMv bP BASE WK KT kP GI xP rP dP IDv sP bB bA xB yP rB xA bD xD BP1 ROW1v rA PASS zP dA ROW0a rD sA ONES dB"
         " sB SEG dD yB yA KEEP1a sD KEEP0v yD zB zA zD").split()
ROUND = ("wrap gP fold gA0 bB+ gA1 bA+ oP oB oA oC mP bP+ cA1 gB0 mA0 mA1 eP cA0 mB0 hA0 gB1 gC0 hA1 cB0 hB0 mB1 mC0 fA gD0 cB1"
         " hB1 cC0 fB gD1 hP hC0 fP xB+ kP+ mD0 mD1 fC cD0 hD0 rB+ cD1 dB+ hD1 xA+ pB sB+ fD rA+ xP+ yB+ zB+ dA+ rP+ dP+ bD+"
         " sA+ yA+ sP+ xD+ rD+ yP+ dD+ zA+ zP+ sD+ yD+ zD+").split()
LAST = ("wrap gP fold gA0 oP mP gA1 gB0 cA1 mA1 mA0 eP cA0 gB1 cB0 hA1 mB0 hA0 gC0 fA gD0 cB1 mB1 hB0 gD1 mC0 cC0 hB1 hC0 fB"
        " mD0 hP fC cD0 mD1 hD0 cD1 fP hD1 fD").split()

SCRATCH = {}
for _names, _spec in [
        ("w0 w1 w2", ("sbuf", [128, M + ROT], "bfloat16")),
        ("res lr", ("sbuf", [128, V], "bfloat16")),
        ("keep", ("sbuf", [128, V], "float16")),
        ("vals", ("sbuf", [128, V * S], "bfloat16")),
        ("his los", ("sbuf", [128, V * S], "float16")),
        ("hb", ("sbuf", [128, RO, 2 * NF], "bfloat16")),
        ("sm sn", ("sbuf", [128, RO, NF], "float16")),
        ("dseg", ("sbuf", [128, NMAX * S + S], "float16")),
        ("band", ("sbuf", [128, 8, 40], "float16")),
        ("wk", ("sbuf", [128, 12, 128], "float16")),
        ("km", ("sbuf", [128, S, 128], "float16")),
        ("kt kp", ("sbuf", [128, RO, 128], "float16")),
        ("pick", ("sbuf", [128, 144], "float16")),
        ("ones", ("sbuf", [128, WIDE], "bfloat16")),
        ("cf", ("sbuf", [128, NF // 16], "float16")),
        ("pi pj", ("sbuf", [128, 4], "int32")),
        ("pf pc", ("sbuf", [128, 8], "float32")),
        ("e5 ee a5 b5 bcol", ("sbuf", [128, 8], "float32")),
        ("n8", ("sbuf", [128, 8], "int32")),
        ("g16 kk bm", ("sbuf", [128, 8, S], "float32")),
        ("jp", ("sbuf", [128, 144], "float32")),
        ("i32 gq", ("sbuf", [128, 128], "float32")),
        ("i16 ih gm gi dn", ("sbuf", [128, 128], "bfloat16")),
        ("in16", ("sbuf", [128, 128], "float16")),
        ("li", ("sbuf", [128, V], "int32")),
        ("ib bp", ("sbuf", [128, RO, S * NF // 16], "float32")),
        ("base", ("sbuf", [128, COLS], "float32")),
        ("zi zj", ("sbuf", [128, COLS], "int32")),
        ("off", ("sbuf", [128, COLS], "uint16")),
        ("mine told", ("sbuf", [128, S * NF // 16], "uint16")),
        ("fP fA fB fC xP xA xB sums", ("psum", [128, 512], "float32"))]:
    for _n in _names.split():
        SCRATCH[_n] = _spec
_chunks = sorted({"%s%d" % (k, i) for gs in GROUPS for k, ns in gs for i in range(len(ns)) if k != "P"})
SEMAPHORES = (["u%d" % i for i in range(60)]
              + [a + c for a in "gc" for c in _chunks] + ["kmv", "kma", "idv", "ida"] + ["gPv", "gPa", "xc", "ev", "wrap", "mP", "es"]
              + [a + k for a in ("fin", "x", "h", "r", "d", "s", "y", "z") for k in "PABD"] + ["finC", "hC"]
              + ["arr0", "arr1", "arr2", "tail0", "tail1", "tail2", "near0", "near1", "near2", "sent", "loadx", "loadp", "loadl",
                 "lists", "stored", "back", "summed"] + ["hand%s%d" % (k, t) for t in range(RO) for k in RELAY[t] + HELPED[t]])

SEGS = [(c5, n8, 15 + 16 * c5 - S * n8) for c5 in range(5) for n8 in range(8) if -15 <= 16 * c5 - S * n8 <= S - 1]


def engine_split(src, peers, topo):
    near = [d for d in peers if d in topo.cores_of(src)]
    far = [d for d in peers if d not in near]
    out = {}
    used = []
    for i, d in enumerate(far):
        es = topo.engines(src, d)
        n = len(es) // len(far)
        out[d] = es[i * n:(i + 1) * n]
        used += es
    for i, d in enumerate(near):
        es = [e for e in topo.engines(src, d) if e not in used]
        n = len(es) // len(near)
        out[d] = es[i * n:(i + 1) * n]
    return out


def mask_of(es):
    return sum(1 << e for e in es)


def meet(a, b):
    return a[0] < b[1] and b[0] < a[1]


def layout():
    spans, chunks = [], []
    for gs in GROUPS:
        n, sp, ch = 0, {}, {}
        for k, ns in gs:
            sp[k] = (n, n + sum(ns))
            for i, a in enumerate(ns):
                ch["%s%d" % (k, i)] = (n, n + a)
                n += a
        spans.append(sp)
        chunks.append(ch)
    return spans, chunks


def sem_of(src, dst, piece, t, T, topo):
    if src == T.cores[-1] and piece[1] == V:
        return "tail%d" % t
    if dst in topo.cores_of(src) and meet(piece, layout()[0][t]["P"]):
        return "near%d" % t
    return "arr%d" % t


def write(g, core, T, topo, moves):
    trs = []
    for d, es, sem, src, dst in moves:
        rid, pid = topo.addr(d, core)
        trs.append(RemoteDMATransfer(dst_ids=[DstId(rid=rid, pnc=pid)], dma_engine_mask=mask_of(es), remote_sem=T.sem[sem], src=src, dst=dst))
    g.remote_dma_fused(trs, local_sem=T.sem.sent)
    return sum(len(m[1]) for m in moves)


def helper_of(core, T, topo):
    return [c for c in topo.cores_of(core) if T.rank_of(c) is None and topo.die(c) == topo.die(core)][0]


def twin_of(core, T, topo):
    return [c for c in T.cores if c not in topo.cores_of(core) and topo.die(c) == topo.die(core)][0]


def helper_program(g, core, T, topo):
    src = twin_of(core, T, topo)
    split = engine_split(core, [c for c in T.cores if c in topo.cores_of(core)], topo)
    sent = 0
    for t, win in ((1, T.w1), (2, T.w2)):
        for k in HELPED[t]:
            piece = layout()[0][t - 1][k]
            at = T.rank_of(src) * V + ROT
            ap = win[:, at + piece[0]:at + piece[1]]
            g.wait_ge(T.sem["hand%s%d" % (k, t)], len(topo.engines(src, core)))
            sent += write(g, core, T, topo, [(d, es, sem_of(src, d, piece, t, T, topo), ap, ap) for d, es in split.items()])
    g.wait_ge(T.sem.sent, sent)


def rank_program(g, core, T, topo):
    rank = T.rank_of(core)
    if rank is None:
        if any(HELPED) and core in [helper_of(c, T, topo) for c in T.cores]:
            helper_program(g, core, T, topo)
        return
    A = AluOpType
    F = ActivationFunctionType
    ve, ac, pe, sy = g.vector, g.scalar, g.tensor, g.sync
    queues = {"g": g, "v": ve, "a": ac, "p": pe, "s": sy}
    count, seen, fresh = {}, {}, [0]

    def done(ins, name=None, n=1):
        if name is None:
            name = "u%d" % fresh[0]
            fresh[0] += 1
        ins.then_inc(T.sem[name], n)
        count[name] = count.get(name, 0) + n
        return (name, count[name])

    def wait(q, *toks):
        for name, n in toks:
            if seen.get((q, name), 0) < n:
                queues[q].wait_ge(T.sem[name], n)
                seen[(q, name)] = n

    peers = [c for c in T.cores if c != core]
    split = engine_split(core, peers, topo)
    lands = {c: len(engine_split(c, [d for d in T.cores if d != c], topo)[core]) for c in peers}
    ender = T.cores[-1]
    mate = [c for c in peers if c in topo.cores_of(core)][0]
    from_mate = len(topo.engines(mate, core))
    own = rank * V
    wins = [T.w0, T.w1, T.w2]
    place = own + ROT
    there = T.rank_of(mate) * V + ROT
    spans, chunks = layout()
    parts = [dict({p: (spans[t][ks[0]][0], spans[t][ks[-1]][1]) for p, ks in PARTS[t].items()}, P=spans[t]["P"]) for t in range(RO)]
    units = [{k: a for k, a in sp.items() if k not in JOIN[t]} for t, sp in enumerate(spans)]
    for t, sp in enumerate(spans):
        units[t]["P"] = (min(sp[k][0] for k in "P" + JOIN[t]), max(sp[k][1] for k in "P" + JOIN[t]))
    pieces = [{"H": (0, HEAD), "R": (HEAD, V), "W": (0, V)}] + units[:-1]
    twin = twin_of(core, T, topo)
    out = [e for d in peers if d != mate for e in split[d]]

    def send(k, t, to=peers):
        piece = pieces[t][k]
        ap = wins[t][:, place + piece[0]:place + piece[1]]
        once = k in RELAY[t] + HELPED[t]
        moves = [(d, split[d], sem_of(core, d, piece, t, T, topo), ap, ap) for d in to if not once or d == mate]
        if once and twin in to:
            moves.append((twin if k in RELAY[t] else helper_of(twin, T, topo), out, "hand%s%d" % (k, t), ap, ap))
        issue(moves)

    def issue(moves):
        count["sent"] = count.get("sent", 0) + write(g, core, T, topo, moves)

    def relay(k, t, es):
        piece, at = pieces[t][k], T.rank_of(twin) * V + ROT
        ap = wins[t][:, at + piece[0]:at + piece[1]]
        wait("g", ("hand%s%d" % (k, t), len(out)))
        return (mate, es, sem_of(twin, mate, piece, t, T, topo), ap, ap)

    def sums(t, es):
        wait("g", tk["e", t])
        count["summed"] = count.get("summed", 0) + len(es)
        tk["summed", t] = ("summed", count["summed"])
        return (mate, es, "summed", T.sm[:, t, 0:NFS[t]], T.sn[:, t, 0:NFS[t]])

    def copy(q, dst, src):
        return ve.tensor_copy(dst, src) if q == "v" else ac.activation(dst, src, F.Identity)

    def plus(q, dst, src, a):
        return ve.tensor_scalar(dst, src, a, None, A.add) if q == "v" else ac.activation(dst, src, F.Identity, bias=a)

    tk, left = {"keep": []}, {}
    for t in range(RO):
        got = {}
        tk["tail", t] = []
        for c in peers:
            for k, piece in pieces[t].items():
                if t == 0 and not any(k == a and ("m" if c == mate else "f") in to for a, to in OPENING):
                    continue
                name, n = sem_of(c, core, piece, t, T, topo), lands[c]
                if k in RELAY[t] and c != mate:
                    name, n = ("hand%s%d" % (k, t), len(out)) if c == twin else (name, lands[mate])
                if k in HELPED[t] and c != mate:
                    n = from_mate // 2
                got[name] = got.get(name, 0) + n
                if c == ender and piece[1] == V:
                    tk["tail", t] = [(name, n)]
        tk["ready", t] = list(got.items())
        tk["near", t] = [("near%d" % t, got["near%d" % t])] if t else []

    t_xp = done(sy.dma_start(T.w0[:, place:place + HEAD], T.x[:, 0:HEAD]), "loadp", 16)
    t_x = done(sy.dma_start(T.w0[:, place + HEAD:place + V], T.x[:, HEAD:V]), "loadx", 16)
    t_l = done(ac.dma_start(T.li[0:8, :], T.liar[:]), "loadl", 16)
    tk["ready", 0] += [t_xp, t_x]
    if core == ender:
        tk["tail", 0] = [t_x]
    fl = {"allow_small_or_imprecise_dtypes": True}
    slot = [NFS.index(n) for n in NFS]

    def fold_base(t):
        w = NFS[t] // 16
        return done(g.iota(T.ib[:, t, 0:S * w], [[KM, S], [(16 * K1) % M, w]], 0, 0, **fl))

    t_pi = done(g.iota(T.pi[:, 0:1], [[0, 1]], 0, 1))
    t_jp = done(g.iota(T.jp[:], [[1, 144]], 0, -1, **fl))
    t_e5 = done(g.iota(T.e5[:, 0:5], [[16, 5]], 0, 0, **fl))
    t_g16 = done(g.iota(T.g16[:], [[16, 8], [0, S]], 0, 0, **fl))
    t_kk = done(g.iota(T.kk[:], [[0, 8], [K5, S]], K2, 0, **fl))
    t_ib = {0: fold_base(0)}
    t_gq = done(g.iota(T.gq[0:8, :], [[1, 8], [0, 16]], 0, -1, **fl))
    for k, to in OPENING:
        wait("g", t_xp, *([] if k == "H" else [t_x]))
        send(k, 0, [d for d in peers if ("m" if d == mate else "f") in to])
    for t in set(slot) - {0}:
        t_ib[t] = fold_base(t)

    unit = 1.0 / M
    step = (8 * K1) % M
    t_z0 = done(ve.memset(T.band[:], 0.0))
    wait("v", t_pi)
    ta = done(ve.tensor_scalar(T.pj[:, 0:1], T.pi[:, 0:1], 15, None, A.bitwise_and), "u59")
    ta = done(ve.tensor_scalar(T.pj[:, 1:2], T.pi[:, 0:1], 112, None, A.bitwise_and), "u59")
    tb = done(ve.tensor_scalar(T.pc[:, 0:1], T.pi[:, 0:1], step * unit, (K1 * own) % M * unit - 0.5, A.mult, A.add))
    wait("v", ta)
    t_pf = done(ve.tensor_copy(T.pf[:, 0:2], T.pj[:, 0:2]))
    wait("v", t_jp)
    t_i32 = done(ve.tensor_scalar(T.i32[:], T.jp[:, 0:128], 0.0, None, A.is_equal))
    wait("v", t_pf, t_e5)
    t_ee = done(ve.tensor_scalar(T.ee[:, 0:5], T.e5[:, 0:5], T.pf[:, 0:1], None, A.add))
    t_pc = done(ve.tensor_scalar(T.pc[:, 2:3], T.pf[:, 0:1], K1 * unit, (K1 * own + K2 * CMID) % M * unit - 0.5,
                                 A.mult, A.add))
    wait("v", t_g16)
    t_bm = done(ve.tensor_scalar(T.bm[:], T.g16[:], T.pf[:, 1:2], unit, A.is_equal, A.mult))
    wait("v", t_ee, tb)
    t_n8 = done(ve.tensor_scalar(T.n8[:, 0:5], T.ee[:, 0:5], -4.5, 0.1, A.add, A.mult))
    t_a5 = done(ve.tensor_scalar(T.a5[:, 0:5], T.ee[:, 0:5], K4 * unit, T.pc[:, 0:1], A.mult, A.add))
    wait("v", t_bm, t_kk, t_z0)
    t_band = done(ve.tensor_tensor(T.band[:, :, 15:15 + S], T.bm[:], T.kk[:], A.mult))
    wait("v", t_n8)
    t_b5 = done(ve.tensor_scalar(T.b5[:, 0:5], T.n8[:, 0:5], (K1 - S * K4) * unit, None, A.mult))
    wait("v", t_a5, t_b5)
    t_bcol = done(ve.tensor_tensor(T.bcol[:, 0:5], T.a5[:, 0:5], T.b5[:, 0:5], A.add))

    def diagonal(q, dst, a, name):
        wait(q, t_i32)
        if q == "v":
            return done(ve.tensor_scalar(dst, T.i32[:], a, None, A.mult), name + "v")
        return done(ac.activation(dst, T.i32[:], F.Identity, scale=a), name + "a")

    def constant(name):
        q = name[-1]
        if name == "WK":
            wait("v", t_band)
            for s, (c5, n8, o) in enumerate(SEGS):
                tk["wk"] = done(ve.tensor_copy(T.wk[:, s, :], T.band[:, :, o:o + 16]), "u56")
        elif name == "PICK":
            tk["pick"] = done(ve.tensor_scalar(T.pick[:], T.jp[:], T.pf[:, 0:1], 15.0, A.add, A.is_equal))
        elif name[:3] == "ROW":
            a = slice(int(name[3]) * V // 2, (int(name[3]) + 1) * V // 2)
            wait(q, t_l)
            tk["row", name[3]] = done(plus(q, T.lr[0:8, a], T.li[0:8, a], 1.0))
        elif name[:2] == "KM":
            for m in range(KM_V) if q == "v" else range(KM_V, S):
                tk["km" + q] = diagonal(q, T.km[:, m, :], (K2 + K5 * m) * unit, "km")
        elif name == "BASE":
            wait("a", t_bcol)
            for c5 in range(5):
                tk["base"] = done(ac.activation(T.base[:, c5::5], T.jp[:, 0:128], F.Identity, bias=T.bcol[:, c5:c5 + 1],
                                                scale=step * unit), "u52")
        elif name[:2] == "BP":
            t = int(q)
            w = S * NFS[t] // 16
            wait("a", t_ib[t], t_pc)
            tk["bp", t] = done(ac.activation(T.bp[:, t, 0:w], T.ib[:, t, 0:w], F.Identity, bias=T.pc[:, 2:3], scale=unit))
        elif name == "KT":
            done(ve.memset(T.kt[0:1, 0, :], (SMID - 7.5) / 16 + UP), "u48")
            for t in range(1, RO):
                done(ve.memset(T.kt[0:1, t, :], K3 * t * unit), "u48")
                tk["kt"] = done(ve.memset(T.kp[0:1, t, :], ((K3 * t + K1 * (there - place + spans[t]["P"][0]) + M // 2) % M - M // 2) * unit),
                                "u48")
        elif name == "PASS":
            if "H" in RELAY[0]:
                issue([relay("H", 0, split[mate])])
        elif name == "ONES":
            done(g.iota(T.dn[0:2, :], [[0, 128]], -MAGIC, MAGIC - UP, **fl), "u58")
            tk["ones"] = done(g.iota(T.ones[0:2, :], [[0, WIDE]], 1, 0, **fl), "u58")
        elif name == "GI":
            wait("v", t_gq)
            for buf, a in ((T.gi, -256.0), (T.gm, float(MAGIC))):
                tk["gi"] = done(ve.tensor_scalar(buf[0:8, :], T.gq[0:8, :], 0.0, a, A.is_equal, A.mult), "u49")
        elif name == "SEG":
            wait("v", done(ve.memset(T.dseg[:], 0.0)))
            tk["d"] = done(ve.memset(T.dseg[:, S - 1::S], RESET))
        elif name[:2] == "ID":
            for buf, a in ((T.ih, 0.5), (T.in16, -1.0 / 16), (T.i16, 1.0 / 16)):
                tk["i16"] = diagonal(q, buf[:], a, "id")
        else:
            a = int(name[4])
            n0, n1 = a * V // 2, (a + 1) * V // 2
            bank, x = [T.fA, T.fB][a][:], T.w0[:, place + n0:place + n1]
            wait("p", tk["gi"], tk["row", name[4]], tk["i16"], t_xp, t_x)
            pe.matmul(bank, T.ih[:], x, True, False)
            pe.matmul(bank, T.ih[:], x, False, False)
            wait(q, done(pe.matmul(bank, T.gi[0:8, :], T.lr[0:8, n0:n1], False, True)))
            tk["keep"].append(done(plus(q, T.keep[:, n0:n1], bank, 512.0)))

    def index_step(s, k, t):
        n0, n1 = parts[t][k]
        c, w = 5 * n0 // 8, 5 * (n1 - n0) // 8
        bank = T.sums if k == "D" else T["x" + k]
        px = bank[:, 0:w]
        wp = w // S
        if s == "b":
            wait("p", t_i32, tk["bp", slot[t]] if k == "P" else tk["base"])
            if k == "D":
                wait("p", tk["ev", t])
            if t:
                wait("p", tk["r", k, t - 1], tk["kt"], tk["ones"])
            pe.matmul(px, T.i32[:], T.bp[:, slot[t], 0:w] if k == "P" else T.base[:, c:c + w], True, False)
            if t:
                pe.matmul(px, (T.kp if k == "P" else T.kt)[0:1, t, :], T.ones[0:1, 0:w], False, False)
            return
        if s == "k":
            wait("p", tk["pick"], *tk["near", t], *([tk["e", t - 1]] if t else [t_xp] if n1 <= HEAD else [t_xp, t_x]))
            at = there if t else place
            for i in range(16):
                ins = pe.matmul(T.sums[:, 0:wp], T.pick[:, 15 - i:143 - i], wins[t][:, at + n0 + i:at + n1:16], i == 0, i == 15)
            wait("a", done(ins, "xc"))
            tk["ev", t] = done(ac.activation(T.cf[:, 0:wp], T.sums[:, 0:wp], F.Identity, bias=-float(CMID)), "ev")
            return
        if s == "x" and k == "P":
            wait("p", tk["ev", t], tk["kmv"], tk["kma"])
            for m in range(S):
                ins = pe.matmul(px[:, m * wp:(m + 1) * wp], T.km[:, m, :], T.cf[:, 0:wp], False, m == S - 1)
        elif s == "x":
            wait("p", tk["wk"], *([tk["f", j, t - 1] for j, a in units[t - 1].items() if meet(a, (n0, n1))] if t else [t_xp, t_x]))
            for i, (c5, n8, o) in enumerate(SEGS):
                ins = pe.matmul(bank[:, c5:w:5], T.wk[:, i, :], wins[t][:, place + n0 + n8:place + n1:8],
                                False, i == len(SEGS) - 1)
        elif s == "r":
            wait("a", tk["x", k, t])
            ins = ac.activation(T.zi[:, c:c + w], px, F.Identity, bias=M / 2, scale=float(M))
        elif s == "d":
            wait("v", tk["r", k, t])
            ins = ve.tensor_scalar(T.zj[:, c:c + w], T.zi[:, c:c + w], M - 1, None, A.bitwise_and)
        elif s == "s":
            wait("a", tk["d", k, t])
            ins = ac.activation(T.zi[:, c:c + w], T.zj[:, c:c + w], F.Square, bias=64.0)
        elif s == "y":
            wait("v", tk["s", k, t])
            ins = ve.tensor_scalar(T.zj[:, c:c + w], T.zi[:, c:c + w], 7, M - 1, A.arith_shift_right, A.bitwise_and)
        else:
            wait(Z_ON[k], tk["y", k, t])
            if t:
                for j, a in chunks[t - 1].items():
                    if meet(a, (n0, n1)):
                        wait(Z_ON[k], *([tk["gPa", t - 1], tk["gPv", t - 1]] if j == "P0" else [tk["g" + j, t - 1]]))
            ins = copy(Z_ON[k], (T.off if t or k != "P" else T.mine)[:, c:c + w], T.zj[:, c:c + w])
        tk[s, k, t] = done(ins, s + k)
        if (s, k, t) == ("z", "P", 0):
            wait("g", tk[s, k, t])
            issue([(mate, split[mate], "lists", T.mine[:, c:c + w], T.told[:, c:c + w])])
            tk[s, k, t] = ("lists", lands[mate])

    def gather(q, lo, hi, t, name):
        src = wins[t][:, 0:M].indirect((T.off if t or name[1] != "P" else T.told)[:, lo // 16:hi // 16])
        dst = T.vals[:, lo:hi]
        wait(q, *[tk["z", p, t] for p, a in parts[t].items() if meet(a, (lo // S, hi // S))], *tk["ready", t])
        tk[name, t] = done(copy(q, dst, src), name)

    def round_step(s, k, t):
        last = t == RO - 1
        win = wins[t]
        grp = k[0:1]
        span = spans[t]
        p0, nf, mv = span["P"][0], NFS[t], MV[t]
        v0 = S * p0

        def close(acc, n0, n, name, stop=True):
            pe.matmul(acc, T.gm[0:8, :], T.lr[0:8, n0:n0 + n], False, False)
            return done(pe.matmul(acc, T.dn[0:2, :], T.ones[0:2, 0:n], False, stop), name)

        if s == "p":
            if k in RELAY[t + 1]:
                issue([relay(k, t + 1, split[mate])])
        elif s == "wrap":
            wait("a", *tk["tail", t])
            tk["ready", t].append(done(ac.activation(win[:, 0:ROT], win[:, M:M + ROT], F.Identity), "wrap"))
        elif s == "g" and k == "P":
            gather("v", v0, v0 + mv * nf, t, "gPv")
            gather("a", v0 + mv * nf, v0 + S * nf, t, "gPa")
        elif s == "fold":
            wait("g", tk["gPv", t], tk["gPa", t])
            rid, pid = topo.addr(mate, core)
            es = topo.engines(core, mate)
            ops = [int(k)] if k else [0, 1]
            h = len(es) // len(ops)
            g.remote_dma_fused([RemoteDMATransfer(
                dst_ids=[DstId(rid=rid, pnc=pid)], dma_engine_mask=mask_of(es[h * j:h * (j + 1)]), remote_sem=T.sem.back,
                srcs=[T.vals[:, v0 + nf * i:v0 + nf * (i + 1)] for i in range(S)],
                dsts=[T.hb[:, t, nf * a:nf * (a + 1)]], alu_op=2 + a) for j, a in enumerate(ops)], local_sem=T.sem.sent)
            count["sent"] += len(es)
            count["back"] = count.get("back", 0) + from_mate
        elif s == "g":
            n0, n1 = chunks[t][k]
            gather("v" if k in BY_VECTOR[t] else "a", S * n0, S * n1, t, "g" + k)
        elif s == "m" and k == "P":
            wait("p", tk["i16"], tk["gPv", t], *([tk["r", "D", t]] if "D" in parts[t] else []))
            for m in range(S):
                if m >= mv:
                    wait("p", tk["gPa", t])
                ins = pe.matmul(T.sums[:, 0:nf], T.i16[:], T.vals[:, v0 + nf * m:v0 + nf * (m + 1)], m == 0, m == S - 1)
            tk["m", k, t] = done(ins, "mP")
        elif s == "e":
            wait("a", tk["m", k, t])
            tk["e", t] = done(ac.activation(T.sm[:, t, 0:nf], T.sums[:, 0:nf], F.Identity, bias=-float(SMID), scale=16.0), "es")
            issue([sums(t, topo.engines(core, mate))])
        elif s == "o":
            a, b = units[t][k]
            acc = T["f" + BANK.get(k, k)][:, 0:b - a]
            wait("p", tk["i16"], *tk["keep"], *([tk["f", j, t - 1] for j in units[t - 1]] if t else []))
            if k in BANK:
                wait("p", tk["f", BANK[k], t])
            left[k, t] = sum(meet(c, (a, b)) for c in chunks[t].values())
            pe.matmul(acc, T.ih[:], win[:, place + a:place + b], True, False)
            if k == "P":
                wait("p", tk["kt"], tk["ones"])
                pe.matmul(acc[:, p0 - a:p0 - a + nf], T.kt[0:1, 0, :], T.ones[0:1, 0:nf], False, False)
        elif s == "h" and k == "P":
            o = p0 - units[t]["P"][0]
            acc = T.fP[:, o:o + nf]
            wait("p", tk["summed", t], ("back", count["back"]))
            pe.matmul(acc, T.i16[:], T.sn[:, t, 0:nf], False, False)
            pe.matmul(acc, T.in16[:], T.hb[:, t, 0:nf], False, False)
            pe.matmul(acc, T.in16[:], T.hb[:, t, nf:2 * nf], False, False)
            left[k, t] -= 1
            tk["h", k, t] = close(acc, p0, nf, "hP", left[k, t] == 0)
        elif s in "mch":
            n0, n1 = chunks[t][k]
            n = n1 - n0
            lo, hi = S * n0, S * n1
            if grp in JOIN[t]:
                grp = "P"
            o = n0 - units[t][grp][0]
            acc = T["f" + BANK.get(grp, grp)][:, o:o + n]
            if s == "m":
                if (grp, t) not in left:
                    round_step("o", grp, t)
                wait("p", tk["g" + k, t])
                for m in range(S):
                    pe.matmul(acc, T.i16[:], T.vals[:, lo + m:hi:S], False, False)
            elif s == "c":
                wait("v", tk["d"], tk["g" + k, t])
                done(ve.tensor_tensor_scan(T.his[:, lo:hi], T.vals[:, lo:hi], T.dseg[:, 0:S * n], 0.0, A.max, A.subtract), "c" + k)
                tk["c", k, t] = done(ve.tensor_tensor_scan(T.los[:, lo:hi], T.dseg[:, S - 1:S - 1 + S * n], T.vals[:, lo:hi],
                                                           0.0, A.max, A.min), "c" + k)
            else:
                wait("p", tk["c", k, t], tk["kt"], tk["ones"])
                pe.matmul(acc, T.in16[:], T.his[:, lo + S - 1:hi:S], False, False)
                pe.matmul(acc, T.in16[:], T.los[:, lo + S - 1:hi:S], False, False)
                left[grp, t] -= 1
                tk["h", grp, t] = close(acc, n0, n, "h" + grp, left[grp, t] == 0)
        else:
            n0, n1 = units[t][k]
            assert left[k, t] == 0
            dst = wins[t + 1][:, place + n0:place + n1] if not last else T.res[:, n0:n1]
            wait("v", tk["h", k, t])
            tf = done(ve.tensor_tensor(dst, T["f" + BANK.get(k, k)][:, 0:n1 - n0], T.keep[:, n0:n1], A.min), "fin" + k)
            tk["f", k, t] = tf
            if last:
                q = "a" if k in STORE_SCALAR else "s"
                wait(q, tf)
                done(queues[q].dma_start(T.y[:, n0:n1], T.res[:, n0:n1]), "stored", 16)
                return
            tk["ready", t + 1].append(tf)
            if core == ender and n1 == V:
                tk["tail", t + 1] = [tf]
            wait("g", tf)
            send(k, t + 1)

    def parse(name):
        for s in ("fold", "wrap"):
            if name.startswith(s):
                return s, name[len(s):]
        return name[0], name[1:]

    for name in FIRST:
        if name[0].isupper():
            constant(name)
        else:
            index_step(*parse(name), 0)
    for t in range(RO):
        for name in ROUND if t + 1 < RO else LAST:
            if name.endswith("+"):
                index_step(*parse(name[:-1]), t + 1)
            else:
                round_step(*parse(name), t)

    wait("s", ("stored", count["stored"]))
    wait("g", ("sent", count["sent"]))
